import numpy as np
import ml_dtypes


def mxq(x, axis, fmt="e4m3"):
    dtype, down = {"e4m3": (ml_dtypes.float8_e4m3fn, 7), "e5m2": (ml_dtypes.float8_e5m2, 14)}[fmt]
    v = np.moveaxis(np.asarray(x, np.float32).astype(ml_dtypes.bfloat16).astype(np.float64), axis, -1)
    blocks = v.reshape(v.shape[:-1] + (-1, 32))
    amax = np.abs(blocks).max(-1, keepdims=True)
    byte = np.maximum(np.where(amax > 0, np.frexp(amax)[1] - 1 + 127, 0) - down, 1)
    scale = np.exp2(byte - 127.0)
    codes = (blocks / scale).astype(np.float32).astype(dtype).astype(np.float64)
    return np.moveaxis((codes * scale).reshape(v.shape), -1, axis)


WIDE = False


def mx_kscale(k):
    if not WIDE:
        return np.ones(k)
    levels = np.array([10, -10, 5, -5, 0])
    if k % 512:
        return np.exp2(np.random.permutation(np.resize(levels, k // 32))).repeat(32)
    a = np.empty((k // 512, 16))
    for p in range(k // 512):
        a[p, :8] = np.random.permutation(np.resize(levels, 8))
        for g in range(8):
            far = levels[np.abs(levels - a[p, g]) >= 10]
            a[p, g + 8] = far[np.random.randint(len(far))]
    return np.exp2(a.ravel()).repeat(32)


def f64(x):
    return np.asarray(x).astype(np.float64)


def striped(idx):
    return np.tile(idx.reshape(-1, 16).T, (8, 1)).astype(np.uint16)


def unstriped(offs):
    return offs[:16].T.reshape(-1).astype(np.int64)


E2M1 = np.array([0.0, 0.5, 1.0, 1.5, 2.0, 3.0, 4.0, 6.0, -0.0, -0.5, -1.0, -1.5, -2.0, -3.0, -4.0, -6.0])


def pack_weight(w, fmt):
    k, n = w.shape
    w = f64(np.asarray(w, np.float32).astype(ml_dtypes.bfloat16)).reshape(k // 32, 32, n)
    amax = np.abs(w).max(1)
    if fmt == "e4m3":
        byte = np.frexp(amax)[1] - 1 + 127 - 7
    else:
        mant, ex = np.frexp(amax / 6.0)
        byte = np.where(mant > 0.5, ex, ex - 1) + 127
    byte = np.clip(np.where(amax > 0, byte, 1), 1, 254)
    scaled = (w * np.exp2(127.0 - byte)[:, None, :]).reshape(k, n).astype(np.float32)
    by_word = np.ascontiguousarray(scaled.reshape(k // 512, 128, 4, n).transpose(0, 1, 3, 2))
    if fmt == "e4m3":
        words = by_word.astype(ml_dtypes.float8_e4m3fn).view(np.uint8)
    else:
        c = by_word.astype(ml_dtypes.float4_e2m1fn).view(np.uint8) & 0xF
        words = (c[..., 0::2] | (c[..., 1::2] << 4)).reshape(k // 512, 128, 2 * n)
    return np.ascontiguousarray(words), np.ascontiguousarray(byte.astype(np.uint8).reshape(k // 512, 16, n))


def unpack_weight(words, scales, fmt):
    g, _, n = scales.shape
    words = np.ascontiguousarray(words).reshape(g, 128, n, -1)
    if fmt == "e4m3":
        vals = words.view(ml_dtypes.float8_e4m3fn).astype(np.float64)
    else:
        nib = np.empty((g, 128, n, 4), np.uint8)
        nib[..., 0::2] = words & 0xF
        nib[..., 1::2] = words >> 4
        vals = E2M1[nib]
    vals = vals * np.repeat(np.exp2(scales.astype(np.float64) - 127.0), 8, axis=1)[..., None]
    return vals.transpose(0, 1, 3, 2).reshape(g * 512, n)


def gelu(v):
    return 0.5 * v * (1.0 + np.tanh(np.sqrt(2.0 / np.pi) * (v + 0.044715 * v**3)))


K, T, E, C, H, N = 1536, 512, 2, 256, 512, 512


def by_expert(wq, xq):
    return np.concatenate([wq[e].T @ xq[:, e * C:(e + 1) * C] for e in range(E)], axis=1)


def setup_inputs():
    n = np.random.standard_normal
    s = mx_kscale(K)
    u = mx_kscale(H)
    slot_token = np.random.permutation(T)[:E * C]
    x = pack_weight(n((K, T)) * s[:, None], "e4m3")
    w1 = [pack_weight(m, "e2m1") for m in n((E, K, H)) / np.sqrt(K) / s[None, :, None]]
    w3 = [pack_weight(m, "e2m1") for m in n((E, K, H)) / np.sqrt(K) / s[None, :, None] * u]
    return {
        "x_words": x[0],
        "x_scales": x[1],
        "w1_words": np.stack([m[0] for m in w1]),
        "w1_scales": np.stack([m[1] for m in w1]),
        "w3_words": np.stack([m[0] for m in w3]),
        "w3_scales": np.stack([m[1] for m in w3]),
        "w2": (n((H, N)) / np.sqrt(H) / u[:, None]).astype(np.float32),
        "gate": np.tile(np.random.uniform(0.2, 1.0, E * C), (128, 1)).astype(np.float32),
        "offs": striped(slot_token),
    }


def reference(x_words, x_scales, w1_words, w1_scales, w3_words, w3_scales, w2, gate, offs):
    w1 = np.stack([unpack_weight(w1_words[e], w1_scales[e], "e2m1") for e in range(E)])
    w3 = np.stack([unpack_weight(w3_words[e], w3_scales[e], "e2m1") for e in range(E)])
    w2q = mxq(f64(w2), 0, "e4m3")
    idx = unstriped(offs)
    xq = unpack_weight(x_words, x_scales, "e4m3")[:, idx]
    h = gelu(by_expert(w1, xq)) * by_expert(w3, xq)
    c = np.zeros((H, T))
    c[:, idx] = f64(gate[:1]) * h
    return w2q.T @ mxq(c, 0, "e4m3")

@@ -1,0 +1,191 @@
+from contextlib import ExitStack
+
+import concourse.mybir as mybir
+from concourse.masks import make_identity
+
+K, T, E, C, H, N = 1536, 512, 2, 256, 512, 512
+FLOPS = 2 * (2 * K * H * E * C + H * N * T)
+
+F32 = mybir.dt.float32
+BF16 = mybir.dt.bfloat16
+I32 = mybir.dt.int32
+U32 = mybir.dt.uint32
+U16 = mybir.dt.uint16
+U8 = mybir.dt.uint8
+FP8X4 = mybir.dt.float8_e4m3fn_x4
+FP4X4 = mybir.dt.float4_e2m1fn_x4
+GELU = mybir.ActivationFunctionType.Gelu_apprx_tanh
+MULT = mybir.AluOpType.mult
+
+P = 128
+PASSES = K // 512
+TILES = E * C // P
+HALF = T // 2
+
+
+def tile_moe_sdn_glu_gelu_kernel(tc, x_words, x_scales, w1_words, w1_scales, w3_words, w3_scales, w2, gate, offs, out):
+    nc = tc.nc
+    with ExitStack() as ctx:
+        keep = ctx.enter_context(tc.tile_pool(name="keep", bufs=1))
+        psum_acc = ctx.enter_context(tc.psum_pool(name="psum_acc", bufs=6))
+        psum_tr = ctx.enter_context(tc.psum_pool(name="psum_tr", bufs=2))
+
+        offsets = keep.tile([P, T // 16], U16, name="offsets")
+        xw0 = keep.tile([P, T], I32, name="xw0", align_bytes=64)
+        xw12 = keep.tile([P, 2, T], I32, name="xw12", align_bytes=64)
+        xw = [xw0[:], xw12[:, 0, :], xw12[:, 1, :]]
+        xs = keep.tile([P, PASSES, T], U8, name="xs", align_bytes=64)
+        ws = [keep.tile([P, E * PASSES, H], U8, name=f"ws{m}", align_bytes=64) for m in range(2)]
+        ww = [[keep.tile([P, PASSES, 2 * H], U8, name=f"ww{m}{e}", align_bytes=64) for e in range(E)] for m in range(2)]
+        gcol = keep.tile([P, TILES], F32, name="gcol")
+        w2raw = keep.tile([P, 4, N], F32, name="w2raw")
+        ident = keep.tile([P, P], F32, name="ident")
+        warm = keep.tile([P, 1], F32, name="warm")
+        warm2 = keep.tile([P, 1], F32, name="warm2")
+
+        nc.vector.memset(xs[:].bitcast(I32), 0)
+        nc.vector.memset(ws[0][:].bitcast(I32), 0)
+        nc.vector.memset(ws[1][:].bitcast(I32), 0)
+        nc.gpsimd.memset(warm[:], 0.0)
+        nc.scalar.activation(warm2[:], warm[:], GELU)
+        make_identity(nc, ident[:])
+
+        def load_scales(m, scales, q):
+            nc.sync.dma_start(ws[m][32 * q : 32 * q + 4].bitcast(I32), scales[:, :, 4 * q : 4 * q + 4, :].rearrange("e s r i -> r (e s) i").bitcast(I32))
+
+        nc.sync.dma_start(offsets[:], offs)
+        nc.sync.dma_start(xw0[:], x_words[0].rearrange("p t d -> p (t d)").bitcast(I32))
+        for q in range(4):
+            nc.sync.dma_start(xs[32 * q : 32 * q + 4].bitcast(I32), x_scales[:, 4 * q : 4 * q + 4, :].rearrange("s r t -> r s t").bitcast(I32))
+        for q in range(4):
+            load_scales(0, w1_scales, q)
+        nc.sync.dma_start(xw12[:], x_words[1:3].rearrange("s p t d -> p s (t d)").bitcast(I32))
+        nc.sync.dma_start(ww[0][0][:].bitcast(I32), w1_words[0].rearrange("s p b -> p s b").bitcast(I32))
+        for q in range(4):
+            load_scales(1, w3_scales, q)
+        nc.sync.dma_start(ww[1][0][:].bitcast(I32), w3_words[0].rearrange("s p b -> p s b").bitcast(I32))
+        with nc.allow_non_contiguous_dma(reason="one gate value a partition"):
+            nc.sync.dma_start(gcol[:], gate[0:1, :].rearrange("o (k p) -> p (o k)", p=P))
+        for m, words in enumerate((w1_words, w3_words)):
+            nc.sync.dma_start(ww[m][1][:].bitcast(I32), words[1].rearrange("s p b -> p s b").bitcast(I32))
+        nc.sync.dma_start(w2raw[:], w2.rearrange("(p j) n -> p j n", j=4))
+
+        gw = [keep.tile([P, T], U32, name=f"gw{s}", align_bytes=64) for s in range(PASSES)]
+        gs = [keep.tile([P, T], U8, name=f"gs{s}", align_bytes=64) for s in range(PASSES)]
+        planes = [keep.tile([P, T], F32, name=f"plane{u}") for u in range(4)]
+        acc = {}
+        turned = [keep.tile([P, 4, C], F32, name=f"turned{e}") for e in range(E)]
+
+        def gather(e, s):
+            lst = offsets[:, e * C // 16 : (e + 1) * C // 16]
+            cols = slice(e * C, (e + 1) * C)
+            nc.vector.tensor_copy(gw[s][:, cols], xw[s].bitcast(U32).indirect(lst))
+            nc.vector.tensor_copy(gs[s][:, cols], xs[:, s, :].indirect(lst))
+
+        def first_layer(k, m, s):
+            e = k * P // C
+            cols = slice(k * P, (k + 1) * P)
+            if s == 0:
+                acc[k, m] = psum_acc.tile([P, H], F32, name="acc")
+            nc.tensor.matmul_mx(
+                out=acc[k, m][:],
+                lhsT=gw[s][:, cols].bitcast(FP8X4),
+                lhsT_scale=gs[s][:, cols],
+                rhs=ww[m][e][:, s, :].bitcast(FP4X4),
+                rhs_scale=ws[m][:, e * PASSES + s, :],
+                start=(s == 0),
+                stop=(s == PASSES - 1),
+            )
+
+        def hidden(k):
+            act = keep.tile([P, 4, P], F32, name=f"act{k}")
+            nc.scalar.activation(act[:], acc[k, 0][:].rearrange("p (m j) -> p j m", j=4), GELU)
+            c_slots = keep.tile([P, 4, P], F32, name=f"c_slots{k}")
+            nc.vector.scalar_tensor_tensor(
+                c_slots[:], act[:], gcol[:, k : k + 1], acc[k, 1][:].rearrange("p (m j) -> p j m", j=4), MULT, MULT
+            )
+            tr = psum_tr.tile([P, 4, P], F32, name="tr")
+            for j in range(4):
+                nc.tensor.transpose(tr[:, j, :], c_slots[:, j, :], ident[:])
+            nc.scalar.copy(turned[k // 2][:, :, (k % 2) * P : (k % 2 + 1) * P], tr[:])
+
+        def scatter(e, j):
+            lst = offsets[:, e * C // 16 : (e + 1) * C // 16]
+            nc.vector.tensor_copy(planes[j][:].indirect(lst), turned[e][:, j, :])
+
+        for s in range(PASSES):
+            gather(0, s)
+            first_layer(0, 0, s)
+            first_layer(1, 0, s)
+        for k in (0, 1):
+            for s in range(PASSES):
+                first_layer(k, 1, s)
+        for s in (0, 1):
+            gather(1, s)
+            for m in range(2):
+                first_layer(2, m, s)
+                first_layer(3, m, s)
+        hidden(0)
+        hidden(1)
+        gather(1, 2)
+        for k in (2, 3):
+            for m in range(2):
+                first_layer(k, m, 2)
+        scatter(0, 0)
+        scatter(0, 1)
+        hidden(2)
+        hidden(3)
+        scatter(0, 2)
+
+        w2b = keep.tile([P, N, 4], BF16, name="w2b", align_bytes=64)
+        for a in range(4):
+            cols = slice(a * P, (a + 1) * P)
+            nc.scalar.copy(w2b[:, cols, :], w2raw[:, :, cols].rearrange("p j n -> p n j"))
+        w2q = keep.tile([P, N], U32, name="w2q", align_bytes=64)
+        w2s = keep.tile([P, N], U8, name="w2s", align_bytes=64)
+
+        cb = [keep.tile([P, HALF, 4], BF16, name=f"cb{h}", align_bytes=64) for h in range(2)]
+
+        def interleave(j, h):
+            src = planes[j][:, h * HALF : (h + 1) * HALF]
+            if j >= 2 and h == 0:
+                nc.vector.tensor_copy(cb[h][:, :, j], src)
+            else:
+                nc.scalar.copy(cb[h][:, :, j], src)
+
+        for j in range(3):
+            scatter(1, j)
+            if j < 2:
+                interleave(j, 0)
+            interleave(j, 1)
+        nc.vector.quantize_mx(out=w2q[:].bitcast(FP8X4), scales=w2s[:], in_=w2b[:].rearrange("p n j -> p (n j)"))
+        scatter(0, 3)
+        interleave(2, 0)
+        scatter(1, 3)
+        interleave(3, 0)
+        interleave(3, 1)
+        cq = [keep.tile([P, HALF], U32, name=f"cq{h}", align_bytes=64) for h in range(2)]
+        cs = [keep.tile([P, HALF], U8, name=f"cs{h}", align_bytes=64) for h in range(2)]
+        for h in range(2):
+            nc.vector.quantize_mx(out=cq[h][:].bitcast(FP8X4), scales=cs[h][:], in_=cb[h][:].rearrange("p t j -> p (t j)"))
+        out_rows = out.rearrange("(a p) t -> p a t", p=P)
+        for h in range(2):
+            for b in range(2):
+                res = psum_acc.tile([P, 2, HALF], F32, name="acc")
+                for j in range(2):
+                    cols = slice((2 * b + j) * P, (2 * b + j + 1) * P)
+                    nc.tensor.matmul_mx(
+                        out=res[:, j, :],
+                        lhsT=w2q[:, cols].bitcast(FP8X4),
+                        lhsT_scale=w2s[:, cols],
+                        rhs=cq[h][:].bitcast(FP8X4),
+                        rhs_scale=cs[h][:],
+                        start=True,
+                        stop=True,
+                    )
+                staged = keep.tile([P, 2, HALF], F32, name=f"staged{h}{b}")
+                if (h, b) in ((0, 0), (0, 1), (1, 1)):
+                    nc.scalar.copy(staged[:], res[:])
+                else:
+                    nc.vector.tensor_copy(staged[:], res[:])
+                nc.sync.dma_start(out_rows[:, 2 * b : 2 * b + 2, h * HALF : (h + 1) * HALF], staged[:])

@@ -15,133 +15,159 @@ U8 = mybir.dt.uint8
 FP8X4 = mybir.dt.float8_e4m3fn_x4
 FP4X4 = mybir.dt.float4_e2m1fn_x4
 GELU = mybir.ActivationFunctionType.Gelu_apprx_tanh
+COPY = mybir.ActivationFunctionType.Copy
 MULT = mybir.AluOpType.mult
 
 P = 128
 PASSES = K // 512
 TILES = E * C // P
 HALF = T // 2
+WARM_PASSES = 5
 
 
 def tile_moe_sdn_glu_gelu_kernel(tc, x_words, x_scales, w1_words, w1_scales, w3_words, w3_scales, w2, gate, offs, out):
     nc = tc.nc
     with ExitStack() as ctx:
         keep = ctx.enter_context(tc.tile_pool(name="keep", bufs=1))
-        psum_acc = ctx.enter_context(tc.psum_pool(name="psum_acc", bufs=6))
-        psum_tr = ctx.enter_context(tc.psum_pool(name="psum_tr", bufs=2))
+        psum_acc = ctx.enter_context(tc.psum_pool(name="psum_acc", bufs=4))
+        psum_tr = ctx.enter_context(tc.psum_pool(name="psum_tr", bufs=4))
 
         offsets = keep.tile([P, T // 16], U16, name="offsets")
-        xw0 = keep.tile([P, T], I32, name="xw0", align_bytes=64)
-        xw12 = keep.tile([P, 2, T], I32, name="xw12", align_bytes=64)
-        xw = [xw0[:], xw12[:, 0, :], xw12[:, 1, :]]
-        xs = keep.tile([P, PASSES, T], U8, name="xs", align_bytes=64)
+        xw = keep.tile([P, PASSES * T], I32, name="xw", align_bytes=64)
+        xs = keep.tile([P, (PASSES + 1) * T], U8, name="xs", align_bytes=64)
         ws = [keep.tile([P, E * PASSES, H], U8, name=f"ws{m}", align_bytes=64) for m in range(2)]
         ww = [[keep.tile([P, PASSES, 2 * H], U8, name=f"ww{m}{e}", align_bytes=64) for e in range(E)] for m in range(2)]
         gcol = keep.tile([P, TILES], F32, name="gcol")
-        w2raw = keep.tile([P, 4, N], F32, name="w2raw")
         ident = keep.tile([P, P], F32, name="ident")
         warm = keep.tile([P, 1], F32, name="warm")
         warm2 = keep.tile([P, 1], F32, name="warm2")
 
-        nc.vector.memset(xs[:].bitcast(I32), 0)
-        nc.vector.memset(ws[0][:].bitcast(I32), 0)
-        nc.vector.memset(ws[1][:].bitcast(I32), 0)
+        nc.vector.memset(xs[:, : 2 * T].bitcast(I32), 0)
+        nc.gpsimd.memset(xs[:, 2 * T :].bitcast(I32), 0)
+        for m in range(2):
+            nc.vector.memset(ws[m][:, 0:PASSES, :].bitcast(I32), 0)
+            nc.gpsimd.memset(ws[m][:, PASSES:, :].bitcast(I32), 0)
         nc.gpsimd.memset(warm[:], 0.0)
         nc.scalar.activation(warm2[:], warm[:], GELU)
         make_identity(nc, ident[:])
 
-        def load_scales(m, scales, q):
-            nc.sync.dma_start(ws[m][32 * q : 32 * q + 4].bitcast(I32), scales[:, :, 4 * q : 4 * q + 4, :].rearrange("e s r i -> r (e s) i").bitcast(I32))
+        def load_tokens(s):
+            nc.sync.dma_start(xw[:, s * T : (s + 1) * T], x_words[s].rearrange("p t d -> p (t d)").bitcast(I32))
+
+        def load_scales(m, scales, r):
+            nc.sync.dma_start(ws[m][r:P:32].bitcast(I32), scales[:, :, r:16:4, :].rearrange("e s q i -> q (e s) i").bitcast(I32))
+
+        def load_weights(m, words, e):
+            nc.sync.dma_start(ww[m][e][:].bitcast(I32), words[e].rearrange("s p b -> p s b").bitcast(I32))
 
         nc.sync.dma_start(offsets[:], offs)
-        nc.sync.dma_start(xw0[:], x_words[0].rearrange("p t d -> p (t d)").bitcast(I32))
-        for q in range(4):
-            nc.sync.dma_start(xs[32 * q : 32 * q + 4].bitcast(I32), x_scales[:, 4 * q : 4 * q + 4, :].rearrange("s r t -> r s t").bitcast(I32))
-        for q in range(4):
-            load_scales(0, w1_scales, q)
-        nc.sync.dma_start(xw12[:], x_words[1:3].rearrange("s p t d -> p s (t d)").bitcast(I32))
-        nc.sync.dma_start(ww[0][0][:].bitcast(I32), w1_words[0].rearrange("s p b -> p s b").bitcast(I32))
-        for q in range(4):
-            load_scales(1, w3_scales, q)
-        nc.sync.dma_start(ww[1][0][:].bitcast(I32), w3_words[0].rearrange("s p b -> p s b").bitcast(I32))
+        load_tokens(0)
+        load_tokens(1)
+        for r in range(4):
+            nc.sync.dma_start(xs[r:P:32, : PASSES * T].bitcast(I32).rearrange("q (s t) -> q s t", s=PASSES), x_scales[:, r:16:4, :].rearrange("s q t -> q s t").bitcast(I32))
+        for m, (words, scales) in enumerate(((w1_words, w1_scales), (w3_words, w3_scales))):
+            load_weights(m, words, 0)
+            for r in range(4):
+                load_scales(m, scales, r)
+        load_tokens(2)
         with nc.allow_non_contiguous_dma(reason="one gate value a partition"):
             nc.sync.dma_start(gcol[:], gate[0:1, :].rearrange("o (k p) -> p (o k)", p=P))
-        for m, words in enumerate((w1_words, w3_words)):
-            nc.sync.dma_start(ww[m][1][:].bitcast(I32), words[1].rearrange("s p b -> p s b").bitcast(I32))
+
+        load_weights(0, w1_words, 1)
+        load_weights(1, w3_words, 1)
+        w2raw = keep.tile([P, 4, N], F32, name="w2raw", tag="w2raw")
         nc.sync.dma_start(w2raw[:], w2.rearrange("(p j) n -> p j n", j=4))
 
-        gw = [keep.tile([P, T], U32, name=f"gw{s}", align_bytes=64) for s in range(PASSES)]
+        gw = {}
         gs = [keep.tile([P, T], U8, name=f"gs{s}", align_bytes=64) for s in range(PASSES)]
-        planes = [keep.tile([P, T], F32, name=f"plane{u}") for u in range(4)]
-        acc = {}
-        turned = [keep.tile([P, 4, C], F32, name=f"turned{e}") for e in range(E)]
 
-        def gather(e, s):
+        def gather_words(e, s):
+            end = (s + 1) * T if e == 0 or s == PASSES - 1 else PASSES * T
             lst = offsets[:, e * C // 16 : (e + 1) * C // 16]
-            cols = slice(e * C, (e + 1) * C)
-            nc.vector.tensor_copy(gw[s][:, cols], xw[s].bitcast(U32).indirect(lst))
-            nc.vector.tensor_copy(gs[s][:, cols], xs[:, s, :].indirect(lst))
+            tag = "act0" if (e, s) == (1, PASSES - 1) else f"gw{e}{s}"
+            gw[e, s] = keep.tile([P, C], U32, name=f"gw{e}{s}", tag=tag, align_bytes=64)
+            nc.vector.tensor_copy(gw[e, s][:], xw[:, s * T : end].bitcast(U32).indirect(lst))
 
-        def first_layer(k, m, s):
+        def gather_scales(s):
+            nc.vector.tensor_copy(gs[s][:], xs[:, s * T : (s + 2) * T].indirect(offsets[:]))
+
+        def first_layer(k, m):
             e = k * P // C
             cols = slice(k * P, (k + 1) * P)
-            if s == 0:
-                acc[k, m] = psum_acc.tile([P, H], F32, name="acc")
-            nc.tensor.matmul_mx(
-                out=acc[k, m][:],
-                lhsT=gw[s][:, cols].bitcast(FP8X4),
-                lhsT_scale=gs[s][:, cols],
-                rhs=ww[m][e][:, s, :].bitcast(FP4X4),
-                rhs_scale=ws[m][:, e * PASSES + s, :],
-                start=(s == 0),
-                stop=(s == PASSES - 1),
-            )
+            acc = psum_acc.tile([P, H], F32, name="acc")
+            order = range(PASSES) if e == 0 else range(PASSES - 1, -1, -1)
+            for s in order:
+                nc.tensor.matmul_mx(
+                    out=acc[:],
+                    lhsT=gw[e, s][:, k % 2 * P : (k % 2 + 1) * P].bitcast(FP8X4),
+                    lhsT_scale=gs[s][:, cols],
+                    rhs=ww[m][e][:, s, :].bitcast(FP4X4),
+                    rhs_scale=ws[m][:, e * PASSES + s, :],
+                    start=(s == order[0]),
+                    stop=(s == order[-1]),
+                )
+            return acc
 
-        def hidden(k):
-            act = keep.tile([P, 4, P], F32, name=f"act{k}")
-            nc.scalar.activation(act[:], acc[k, 0][:].rearrange("p (m j) -> p j m", j=4), GELU)
-            c_slots = keep.tile([P, 4, P], F32, name=f"c_slots{k}")
-            nc.vector.scalar_tensor_tensor(
-                c_slots[:], act[:], gcol[:, k : k + 1], acc[k, 1][:].rearrange("p (m j) -> p j m", j=4), MULT, MULT
-            )
+        def turn(factor, pieces):
             tr = psum_tr.tile([P, 4, P], F32, name="tr")
             for j in range(4):
-                nc.tensor.transpose(tr[:, j, :], c_slots[:, j, :], ident[:])
-            nc.scalar.copy(turned[k // 2][:, :, (k % 2) * P : (k % 2 + 1) * P], tr[:])
+                nc.tensor.transpose(tr[:, j, :], factor[:, j, :], ident[:])
+            for lo, hi, dst in pieces:
+                nc.scalar.copy(dst, tr[:, lo:hi, :])
+            return tr
 
-        def scatter(e, j):
-            lst = offsets[:, e * C // 16 : (e + 1) * C // 16]
-            nc.vector.tensor_copy(planes[j][:].indirect(lst), turned[e][:, j, :])
+        def by_plane(acc):
+            return acc[:].rearrange("p (q j) -> p j q", j=4)
+
+        def slots(lo, hi):
+            return offsets[:, lo * P // 16 : hi * P // 16]
 
         for s in range(PASSES):
-            gather(0, s)
-            first_layer(0, 0, s)
-            first_layer(1, 0, s)
-        for k in (0, 1):
-            for s in range(PASSES):
-                first_layer(k, 1, s)
-        for s in (0, 1):
-            gather(1, s)
-            for m in range(2):
-                first_layer(2, m, s)
-                first_layer(3, m, s)
-        hidden(0)
-        hidden(1)
-        gather(1, 2)
-        for k in (2, 3):
-            for m in range(2):
-                first_layer(k, m, 2)
-        scatter(0, 0)
-        scatter(0, 1)
-        hidden(2)
-        hidden(3)
-        scatter(0, 2)
+            gather_words(0, s)
+            gather_scales(s)
+        for s in range(PASSES - 1):
+            gather_words(1, s)
+
+        def hidden(k):
+            act = keep.tile([P, 4, P], F32, name=f"act{k}", tag=f"act{k}", align_bytes=64)
+            nc.scalar.activation(act[:], by_plane(first_layer(k, 0)), GELU)
+            c_slots = keep.tile([P, 4, P], F32, name=f"c_slots{k}")
+            nc.vector.scalar_tensor_tensor(c_slots[:], act[:], gcol[:, k : k + 1], by_plane(first_layer(k, 1)), MULT, MULT)
+            return c_slots
+
+        def scatter(j, lst, src):
+            nc.vector.tensor_copy(planes[j][:].indirect(lst), src)
+
+        planes = [keep.tile([P, T], F32, name=f"plane{j}") for j in range(2)]
+        rows = [hidden(0), hidden(1)]
+        gather_words(1, PASSES - 1)
+        low0 = keep.tile([P, 2, C], F32, name="low0")
+        high0 = keep.tile([P, 2, C], F32, name="high0")
+        for k in range(2):
+            cols = slice(k * P, (k + 1) * P)
+            turn(rows[k], [(0, 2, low0[:, :, cols]), (2, 4, high0[:, :, cols])])
+            for j in range(2):
+                scatter(j, slots(k, k + 1), low0[:, j, cols])
 
         w2b = keep.tile([P, N, 4], BF16, name="w2b", align_bytes=64)
         for a in range(4):
             cols = slice(a * P, (a + 1) * P)
-            nc.scalar.copy(w2b[:, cols, :], w2raw[:, :, cols].rearrange("p j n -> p n j"))
-        w2q = keep.tile([P, N], U32, name="w2q", align_bytes=64)
+            nc.scalar.copy(
+                w2b[:, cols, :].rearrange("p (c i) j -> p c j i", i=4),
+                w2raw[:, :, cols].rearrange("p j (c i) -> p c j i", i=4),
+            )
+        low1 = keep.tile([P, 2, C], F32, name="low1", tag="low1", align_bytes=64)
+        third = keep.tile([P, 1, C], F32, name="third", tag="w2raw")
+        held = []
+        for k in (2, 3):
+            cols = slice((k - 2) * P, (k - 1) * P)
+            held.append(turn(hidden(k), [(0, 2, low1[:, :, cols]), (2, 3, third[:, :, cols])]))
+            planes.append(keep.tile([P, T], F32, name=f"plane{k}", tag=f"act{k}", align_bytes=64))
+            scatter(k, slots(0, 2), high0[:, k - 2, :])
+        for j in range(2):
+            scatter(j, slots(2, 4), low1[:, j, :])
+
+        w2q = keep.tile([P, N], U32, name="w2q", tag="low1", align_bytes=64)
         w2s = keep.tile([P, N], U8, name="w2s", align_bytes=64)
 
         cb = [keep.tile([P, HALF, 4], BF16, name=f"cb{h}", align_bytes=64) for h in range(2)]
@@ -153,39 +179,45 @@ def tile_moe_sdn_glu_gelu_kernel(tc, x_words, x_scales, w1_words, w1_scales, w3_
             else:
                 nc.scalar.copy(cb[h][:, :, j], src)
 
-        for j in range(3):
-            scatter(1, j)
-            if j < 2:
-                interleave(j, 0)
+        for j in range(2):
+            interleave(j, 0)
             interleave(j, 1)
         nc.vector.quantize_mx(out=w2q[:].bitcast(FP8X4), scales=w2s[:], in_=w2b[:].rearrange("p n j -> p (n j)"))
-        scatter(0, 3)
+        idle = psum_tr.tile([P, N], F32, name="tr")
+        for r in range(WARM_PASSES):
+            nc.tensor.matmul_mx(
+                out=idle[:], lhsT=w2q[:, 0:P].bitcast(FP8X4), lhsT_scale=w2s[:, 0:P],
+                rhs=w2q[:].bitcast(FP8X4), rhs_scale=w2s[:], start=True, stop=True,
+            )
+        scatter(2, slots(2, 4), third[:, 0, :])
+        fourth = keep.tile([P, C], F32, name="fourth", tag="w2raw")
+        for i in range(2):
+            nc.scalar.copy(fourth[:, i * P : (i + 1) * P], held[i][:, 3, :])
+        interleave(2, 1)
         interleave(2, 0)
-        scatter(1, 3)
+        scatter(3, slots(2, 4), fourth[:])
         interleave(3, 0)
         interleave(3, 1)
         cq = [keep.tile([P, HALF], U32, name=f"cq{h}", align_bytes=64) for h in range(2)]
         cs = [keep.tile([P, HALF], U8, name=f"cs{h}", align_bytes=64) for h in range(2)]
         for h in range(2):
             nc.vector.quantize_mx(out=cq[h][:].bitcast(FP8X4), scales=cs[h][:], in_=cb[h][:].rearrange("p t j -> p (t j)"))
-        out_rows = out.rearrange("(a p) t -> p a t", p=P)
         for h in range(2):
-            for b in range(2):
-                res = psum_acc.tile([P, 2, HALF], F32, name="acc")
-                for j in range(2):
-                    cols = slice((2 * b + j) * P, (2 * b + j + 1) * P)
-                    nc.tensor.matmul_mx(
-                        out=res[:, j, :],
-                        lhsT=w2q[:, cols].bitcast(FP8X4),
-                        lhsT_scale=w2s[:, cols],
-                        rhs=cq[h][:].bitcast(FP8X4),
-                        rhs_scale=cs[h][:],
-                        start=True,
-                        stop=True,
-                    )
-                staged = keep.tile([P, 2, HALF], F32, name=f"staged{h}{b}")
-                if (h, b) in ((0, 0), (0, 1), (1, 1)):
+            for a in range(4):
+                res = psum_tr.tile([P, HALF], F32, name="tr") if h else psum_acc.tile([P, HALF], F32, name="acc")
+                cols = slice(a * P, (a + 1) * P)
+                nc.tensor.matmul_mx(
+                    out=res[:],
+                    lhsT=w2q[:, cols].bitcast(FP8X4),
+                    lhsT_scale=w2s[:, cols],
+                    rhs=cq[h][:].bitcast(FP8X4),
+                    rhs_scale=cs[h][:],
+                    start=True,
+                    stop=True,
+                )
+                staged = keep.tile([P, HALF], F32, name=f"staged{h}{a}")
+                if a % 2 == 0:
                     nc.scalar.copy(staged[:], res[:])
                 else:
                     nc.vector.tensor_copy(staged[:], res[:])
-                nc.sync.dma_start(out_rows[:, 2 * b : 2 * b + 2, h * HALF : (h + 1) * HALF], staged[:])
+                nc.sync.dma_start(out[cols, h * HALF : (h + 1) * HALF], staged[:])

@@ -29,8 +29,8 @@ def tile_moe_sdn_glu_gelu_kernel(tc, x_words, x_scales, w1_words, w1_scales, w3_
     nc = tc.nc
     with ExitStack() as ctx:
         keep = ctx.enter_context(tc.tile_pool(name="keep", bufs=1))
-        psum_acc = ctx.enter_context(tc.psum_pool(name="psum_acc", bufs=4))
-        psum_tr = ctx.enter_context(tc.psum_pool(name="psum_tr", bufs=4))
+        psum_acc = ctx.enter_context(tc.psum_pool(name="psum_acc", bufs=3))
+        psum_tr = ctx.enter_context(tc.psum_pool(name="psum_tr", bufs=5))
 
         offsets = keep.tile([P, T // 16], U16, name="offsets")
         xw = keep.tile([P, PASSES * T], I32, name="xw", align_bytes=64)
@@ -149,21 +149,23 @@ def tile_moe_sdn_glu_gelu_kernel(tc, x_words, x_scales, w1_words, w1_scales, w3_
             for j in range(2):
                 scatter(j, slots(k, k + 1), low0[:, j, cols])
 
-        w2b = keep.tile([P, N, 4], BF16, name="w2b", align_bytes=64)
+        low1 = keep.tile([P, 2, C], F32, name="low1", tag="low1", align_bytes=64)
+        held = []
+        for k in (2, 3):
+            cols = slice((k - 2) * P, (k - 1) * P)
+            held.append(turn(hidden(k), [(0, 2, low1[:, :, cols])]))
+            planes.append(keep.tile([P, T], F32, name=f"plane{k}", tag=f"act{k}", align_bytes=64))
+            scatter(k, slots(0, 2), high0[:, k - 2, :])
+        w2b = keep.tile([P, N, 4], BF16, name="w2b", tag="gw10", align_bytes=64)
         for a in range(4):
             cols = slice(a * P, (a + 1) * P)
             nc.scalar.copy(
                 w2b[:, cols, :].rearrange("p (c i) j -> p c j i", i=4),
                 w2raw[:, :, cols].rearrange("p j (c i) -> p c j i", i=4),
             )
-        low1 = keep.tile([P, 2, C], F32, name="low1", tag="low1", align_bytes=64)
-        third = keep.tile([P, 1, C], F32, name="third", tag="w2raw")
-        held = []
-        for k in (2, 3):
-            cols = slice((k - 2) * P, (k - 1) * P)
-            held.append(turn(hidden(k), [(0, 2, low1[:, :, cols]), (2, 3, third[:, :, cols])]))
-            planes.append(keep.tile([P, T], F32, name=f"plane{k}", tag=f"act{k}", align_bytes=64))
-            scatter(k, slots(0, 2), high0[:, k - 2, :])
+        third = keep.tile([P, C], F32, name="third", tag="w2raw")
+        for i in range(2):
+            nc.scalar.copy(third[:, i * P : (i + 1) * P], held[i][:, 2, :])
         for j in range(2):
             scatter(j, slots(2, 4), low1[:, j, :])
 
@@ -189,22 +191,23 @@ def tile_moe_sdn_glu_gelu_kernel(tc, x_words, x_scales, w1_words, w1_scales, w3_
                 out=idle[:], lhsT=w2q[:, 0:P].bitcast(FP8X4), lhsT_scale=w2s[:, 0:P],
                 rhs=w2q[:].bitcast(FP8X4), rhs_scale=w2s[:], start=True, stop=True,
             )
-        scatter(2, slots(2, 4), third[:, 0, :])
+        scatter(2, slots(2, 4), third[:])
         fourth = keep.tile([P, C], F32, name="fourth", tag="w2raw")
         for i in range(2):
             nc.scalar.copy(fourth[:, i * P : (i + 1) * P], held[i][:, 3, :])
         interleave(2, 1)
         interleave(2, 0)
         scatter(3, slots(2, 4), fourth[:])
-        interleave(3, 0)
         interleave(3, 1)
+        for i in range(2):
+            nc.vector.tensor_copy(cb[0][:, i * P : (i + 1) * P, 3], planes[3][:, i * P : (i + 1) * P])
         cq = [keep.tile([P, HALF], U32, name=f"cq{h}", align_bytes=64) for h in range(2)]
         cs = [keep.tile([P, HALF], U8, name=f"cs{h}", align_bytes=64) for h in range(2)]
-        for h in range(2):
-            nc.vector.quantize_mx(out=cq[h][:].bitcast(FP8X4), scales=cs[h][:], in_=cb[h][:].rearrange("p t j -> p (t j)"))
+        for h, lo, hi in ((0, 0, P), (0, P, HALF), (1, 0, HALF)):
+            nc.vector.quantize_mx(out=cq[h][:, lo:hi].bitcast(FP8X4), scales=cs[h][:, lo:hi], in_=cb[h][:, lo:hi, :].rearrange("p t j -> p (t j)"))
         for h in range(2):
             for a in range(4):
-                res = psum_tr.tile([P, HALF], F32, name="tr") if h else psum_acc.tile([P, HALF], F32, name="acc")
+                res = psum_tr.tile([P, HALF], F32, name="tr") if 4 * h + a >= 3 else psum_acc.tile([P, HALF], F32, name="acc")
                 cols = slice(a * P, (a + 1) * P)
                 nc.tensor.matmul_mx(
                     out=res[:],

@@ -35,27 +35,29 @@ def tile_moe_sdn_glu_gelu_kernel(tc, x_words, x_scales, w1_words, w1_scales, w3_
         offsets = keep.tile([P, T // 16], U16, name="offsets")
         xw = keep.tile([P, PASSES * T], I32, name="xw", align_bytes=64)
         xs = keep.tile([P, (PASSES + 1) * T], U8, name="xs", align_bytes=64)
-        ws = [keep.tile([P, E * PASSES, H], U8, name=f"ws{m}", align_bytes=64) for m in range(2)]
+        ws = [[keep.tile([P, PASSES, H], U8, name=f"ws{m}0", align_bytes=64)] for m in range(2)]
         ww = [[keep.tile([P, PASSES, 2 * H], U8, name=f"ww{m}{e}", align_bytes=64) for e in range(E)] for m in range(2)]
         gcol = keep.tile([P, TILES], F32, name="gcol")
         ident = keep.tile([P, P], F32, name="ident")
-        warm = keep.tile([P, 1], F32, name="warm")
-        warm2 = keep.tile([P, 1], F32, name="warm2")
+        warm = [keep.tile([P, 1], F32, name=f"warm{m}", tag=f"warm{m}", align_bytes=64) for m in range(2)]
 
         nc.vector.memset(xs[:, : 2 * T].bitcast(I32), 0)
         nc.gpsimd.memset(xs[:, 2 * T :].bitcast(I32), 0)
         for m in range(2):
-            nc.vector.memset(ws[m][:, 0:PASSES, :].bitcast(I32), 0)
-            nc.gpsimd.memset(ws[m][:, PASSES:, :].bitcast(I32), 0)
-        nc.gpsimd.memset(warm[:], 0.0)
-        nc.scalar.activation(warm2[:], warm[:], GELU)
+            nc.vector.memset(ws[m][0][:].bitcast(I32), 0)
+        nc.gpsimd.memset(warm[0][:], 0.0)
+        nc.scalar.activation(warm[1][:], warm[0][:], GELU)
         make_identity(nc, ident[:])
+        for m in range(2):
+            ws[m].append(keep.tile([P, PASSES, H], U8, name=f"ws{m}1", tag=f"warm{m}", align_bytes=64))
+            nc.gpsimd.memset(ws[m][1][:].bitcast(I32), 0)
 
         def load_tokens(s):
             nc.sync.dma_start(xw[:, s * T : (s + 1) * T], x_words[s].rearrange("p t d -> p (t d)").bitcast(I32))
 
-        def load_scales(m, scales, r):
-            nc.sync.dma_start(ws[m][r:P:32].bitcast(I32), scales[:, :, r:16:4, :].rearrange("e s q i -> q (e s) i").bitcast(I32))
+        def load_scales(m, scales, e):
+            for r in range(4):
+                nc.sync.dma_start(ws[m][e][r:P:32].bitcast(I32), scales[e, :, r:16:4, :].rearrange("s q i -> q s i").bitcast(I32))
 
         def load_weights(m, words, e):
             nc.sync.dma_start(ww[m][e][:].bitcast(I32), words[e].rearrange("s p b -> p s b").bitcast(I32))
@@ -65,16 +67,18 @@ def tile_moe_sdn_glu_gelu_kernel(tc, x_words, x_scales, w1_words, w1_scales, w3_
         load_tokens(1)
         for r in range(4):
             nc.sync.dma_start(xs[r:P:32, : PASSES * T].bitcast(I32).rearrange("q (s t) -> q s t", s=PASSES), x_scales[:, r:16:4, :].rearrange("s q t -> q s t").bitcast(I32))
-        for m, (words, scales) in enumerate(((w1_words, w1_scales), (w3_words, w3_scales))):
-            load_weights(m, words, 0)
-            for r in range(4):
-                load_scales(m, scales, r)
+        load_weights(0, w1_words, 0)
+        load_scales(0, w1_scales, 0)
+        load_weights(1, w3_words, 0)
+        load_scales(1, w3_scales, 0)
         load_tokens(2)
         with nc.allow_non_contiguous_dma(reason="one gate value a partition"):
             nc.sync.dma_start(gcol[:], gate[0:1, :].rearrange("o (k p) -> p (o k)", p=P))
 
         load_weights(0, w1_words, 1)
+        load_scales(0, w1_scales, 1)
         load_weights(1, w3_words, 1)
+        load_scales(1, w3_scales, 1)
         w2raw = keep.tile([P, 4, N], F32, name="w2raw", tag="w2raw")
         nc.sync.dma_start(w2raw[:], w2.rearrange("(p j) n -> p j n", j=4))
 
@@ -102,7 +106,7 @@ def tile_moe_sdn_glu_gelu_kernel(tc, x_words, x_scales, w1_words, w1_scales, w3_
                     lhsT=gw[e, s][:, k % 2 * P : (k % 2 + 1) * P].bitcast(FP8X4),
                     lhsT_scale=gs[s][:, cols],
                     rhs=ww[m][e][:, s, :].bitcast(FP4X4),
-                    rhs_scale=ws[m][:, e * PASSES + s, :],
+                    rhs_scale=ws[m][e][:, s, :],
                     start=(s == order[0]),
                     stop=(s == order[-1]),
                 )

@@ -15,216 +15,196 @@ U8 = mybir.dt.uint8
 FP8X4 = mybir.dt.float8_e4m3fn_x4
 FP4X4 = mybir.dt.float4_e2m1fn_x4
 GELU = mybir.ActivationFunctionType.Gelu_apprx_tanh
-COPY = mybir.ActivationFunctionType.Copy
 MULT = mybir.AluOpType.mult
 
 P = 128
 PASSES = K // 512
 TILES = E * C // P
 HALF = T // 2
-WARM_PASSES = 5
+WARM_PASSES = 4
 
 
 def tile_moe_sdn_glu_gelu_kernel(tc, x_words, x_scales, w1_words, w1_scales, w3_words, w3_scales, w2, gate, offs, out):
     nc = tc.nc
     with ExitStack() as ctx:
         keep = ctx.enter_context(tc.tile_pool(name="keep", bufs=1))
-        psum_acc = ctx.enter_context(tc.psum_pool(name="psum_acc", bufs=3))
-        psum_tr = ctx.enter_context(tc.psum_pool(name="psum_tr", bufs=5))
+        early = ctx.enter_context(tc.tile_pool(name="early", bufs=1))
+        psum_acc = ctx.enter_context(tc.psum_pool(name="psum_acc", bufs=6))
+        psum_tr = ctx.enter_context(tc.psum_pool(name="psum_tr", bufs=1))
 
         offsets = keep.tile([P, T // 16], U16, name="offsets")
-        xw = keep.tile([P, PASSES * T], I32, name="xw", align_bytes=64)
-        xs = keep.tile([P, (PASSES + 1) * T], U8, name="xs", align_bytes=64)
-        ws = [[keep.tile([P, PASSES, H], U8, name=f"ws{m}0", align_bytes=64)] for m in range(2)]
-        ww = [[keep.tile([P, PASSES, 2 * H], U8, name=f"ww{m}{e}", align_bytes=64) for e in range(E)] for m in range(2)]
+        xw = early.tile([P, PASSES * T], I32, name="xw", offset=0, align_bytes=64)
+        xs = keep.tile([P, PASSES * T], U8, name="xs", align_bytes=64)
+        ws = [[keep.tile([P, PASSES, H], U8, name=f"ws{m}{e}", align_bytes=64) for e in range(E)] for m in range(2)]
+        ww = [[keep.tile([P, PASSES, 2 * H], U8, name=f"ww{m}{e}", tag=f"ww{m}{e}", align_bytes=64) for e in range(E)] for m in range(2)]
         gcol = keep.tile([P, TILES], F32, name="gcol")
         ident = keep.tile([P, P], F32, name="ident")
-        warm = [keep.tile([P, 1], F32, name=f"warm{m}", tag=f"warm{m}", align_bytes=64) for m in range(2)]
+        warm = [keep.tile([P, 1], F32, name=f"warm{m}") for m in range(2)]
 
-        nc.vector.memset(xs[:, : 2 * T].bitcast(I32), 0)
-        nc.gpsimd.memset(xs[:, 2 * T :].bitcast(I32), 0)
-        for m in range(2):
-            nc.vector.memset(ws[m][0][:].bitcast(I32), 0)
+        nc.gpsimd.memset(xs[:].bitcast(I32), 0)
+        for e in range(E):
+            for m in range(2):
+                nc.vector.memset(ws[m][e][:].bitcast(I32), 0)
         nc.gpsimd.memset(warm[0][:], 0.0)
         nc.scalar.activation(warm[1][:], warm[0][:], GELU)
         make_identity(nc, ident[:])
-        for m in range(2):
-            ws[m].append(keep.tile([P, PASSES, H], U8, name=f"ws{m}1", tag=f"warm{m}", align_bytes=64))
-            nc.gpsimd.memset(ws[m][1][:].bitcast(I32), 0)
 
-        def load_tokens(s):
-            nc.sync.dma_start(xw[:, s * T : (s + 1) * T], x_words[s].rearrange("p t d -> p (t d)").bitcast(I32))
+        def load_tokens(lo, hi):
+            nc.sync.dma_start(
+                xw[:, lo * T : hi * T].rearrange("p (s t) -> p s t", t=T),
+                x_words[lo:hi].rearrange("s p t d -> p s (t d)").bitcast(I32),
+            )
 
-        def load_scales(m, scales, e):
+        def load_matrix(m, e):
+            words, scales = ((w1_words, w1_scales), (w3_words, w3_scales))[m]
+            nc.sync.dma_start(ww[m][e][:].bitcast(I32), words[e].rearrange("s p b -> p s b").bitcast(I32))
             for r in range(4):
                 nc.sync.dma_start(ws[m][e][r:P:32].bitcast(I32), scales[e, :, r:16:4, :].rearrange("s q i -> q s i").bitcast(I32))
 
-        def load_weights(m, words, e):
-            nc.sync.dma_start(ww[m][e][:].bitcast(I32), words[e].rearrange("s p b -> p s b").bitcast(I32))
-
         nc.sync.dma_start(offsets[:], offs)
-        load_tokens(0)
-        load_tokens(1)
+        load_tokens(0, 1)
         for r in range(4):
-            nc.sync.dma_start(xs[r:P:32, : PASSES * T].bitcast(I32).rearrange("q (s t) -> q s t", s=PASSES), x_scales[:, r:16:4, :].rearrange("s q t -> q s t").bitcast(I32))
-        load_weights(0, w1_words, 0)
-        load_scales(0, w1_scales, 0)
-        load_weights(1, w3_words, 0)
-        load_scales(1, w3_scales, 0)
-        load_tokens(2)
+            nc.sync.dma_start(xs[r:P:32].bitcast(I32).rearrange("q (s t) -> q s t", s=PASSES), x_scales[:, r:16:4, :].rearrange("s q t -> q s t").bitcast(I32))
+        load_tokens(1, PASSES)
+        load_matrix(0, 0)
+        load_matrix(1, 0)
+        load_matrix(0, 1)
         with nc.allow_non_contiguous_dma(reason="one gate value a partition"):
             nc.sync.dma_start(gcol[:], gate[0:1, :].rearrange("o (k p) -> p (o k)", p=P))
-
-        load_weights(0, w1_words, 1)
-        load_scales(0, w1_scales, 1)
-        load_weights(1, w3_words, 1)
-        load_scales(1, w3_scales, 1)
-        w2raw = keep.tile([P, 4, N], F32, name="w2raw", tag="w2raw")
+        w2raw = keep.tile([P, 4, N], F32, name="w2raw")
         nc.sync.dma_start(w2raw[:], w2.rearrange("(p j) n -> p j n", j=4))
+        load_matrix(1, 1)
 
         gw = {}
-        gs = [keep.tile([P, T], U8, name=f"gs{s}", align_bytes=64) for s in range(PASSES)]
-
-        def gather_words(e, s):
-            end = (s + 1) * T if e == 0 or s == PASSES - 1 else PASSES * T
-            lst = offsets[:, e * C // 16 : (e + 1) * C // 16]
-            tag = "act0" if (e, s) == (1, PASSES - 1) else f"gw{e}{s}"
-            gw[e, s] = keep.tile([P, C], U32, name=f"gw{e}{s}", tag=tag, align_bytes=64)
-            nc.vector.tensor_copy(gw[e, s][:], xw[:, s * T : end].bitcast(U32).indirect(lst))
-
-        def gather_scales(s):
-            nc.vector.tensor_copy(gs[s][:], xs[:, s * T : (s + 2) * T].indirect(offsets[:]))
-
-        def first_layer(k, m):
-            e = k * P // C
-            cols = slice(k * P, (k + 1) * P)
-            acc = psum_acc.tile([P, H], F32, name="acc")
-            order = range(PASSES) if e == 0 else range(PASSES - 1, -1, -1)
-            for s in order:
-                nc.tensor.matmul_mx(
-                    out=acc[:],
-                    lhsT=gw[e, s][:, k % 2 * P : (k % 2 + 1) * P].bitcast(FP8X4),
-                    lhsT_scale=gs[s][:, cols],
-                    rhs=ww[m][e][:, s, :].bitcast(FP4X4),
-                    rhs_scale=ws[m][e][:, s, :],
-                    start=(s == order[0]),
-                    stop=(s == order[-1]),
-                )
-            return acc
-
-        def turn(factor, pieces):
-            tr = psum_tr.tile([P, 4, P], F32, name="tr")
-            for j in range(4):
-                nc.tensor.transpose(tr[:, j, :], factor[:, j, :], ident[:])
-            for lo, hi, dst in pieces:
-                nc.scalar.copy(dst, tr[:, lo:hi, :])
-            return tr
-
-        def by_plane(acc):
-            return acc[:].rearrange("p (q j) -> p j q", j=4)
+        gs = {}
 
         def slots(lo, hi):
             return offsets[:, lo * P // 16 : hi * P // 16]
 
-        for s in range(PASSES):
-            gather_words(0, s)
-            gather_scales(s)
-        for s in range(PASSES - 1):
-            gather_words(1, s)
+        def gather_words(e, s):
+            end = (s + 1) * T if e == 0 or s == PASSES - 1 else PASSES * T
+            gw[e, s] = keep.tile([P, C], U32, name=f"gw{e}{s}", align_bytes=64)
+            nc.vector.tensor_copy(gw[e, s][:], xw[:, s * T : end].bitcast(U32).indirect(slots(2 * e, 2 * e + 2)))
 
-        def hidden(k):
-            act = keep.tile([P, 4, P], F32, name=f"act{k}", tag=f"act{k}", align_bytes=64)
-            nc.scalar.activation(act[:], by_plane(first_layer(k, 0)), GELU)
-            c_slots = keep.tile([P, 4, P], F32, name=f"c_slots{k}")
-            nc.vector.scalar_tensor_tensor(c_slots[:], act[:], gcol[:, k : k + 1], by_plane(first_layer(k, 1)), MULT, MULT)
+        def gather_scales(e, s, dst):
+            gs[e, s] = dst
+            nc.vector.tensor_copy(dst[:], xs[:, s * T : (s + 1) * T].indirect(slots(2 * e, 2 * e + 2)))
+
+        def first_layer(e):
+            acc = {(k, m): psum_acc.tile([P, H], F32, name="acc") for m in range(2) for k in range(2)}
+            for m in range(2):
+                for s in range(PASSES):
+                    for k in range(2):
+                        nc.tensor.matmul_mx(
+                            out=acc[k, m][:],
+                            lhsT=gw[e, s][:, k * P : (k + 1) * P].bitcast(FP8X4),
+                            lhsT_scale=gs[e, s][:, k * P : (k + 1) * P],
+                            rhs=ww[m][e][:, s, :].bitcast(FP4X4),
+                            rhs_scale=ws[m][e][:, s, :],
+                            start=(s == 0),
+                            stop=(s == PASSES - 1),
+                        )
+            return acc
+
+        def hidden(acc, k, tag):
+            act = keep.tile([P, H], F32, name=f"act{k}", tag=f"act{k}", align_bytes=64)
+            nc.scalar.activation(act[:], acc[k % 2, 0][:], GELU)
+            c_slots = keep.tile([P, H], BF16, name=f"c_slots{k}", tag=tag, align_bytes=64)
+            nc.vector.scalar_tensor_tensor(c_slots[:], act[:], gcol[:, k : k + 1], acc[k % 2, 1][:], MULT, MULT)
             return c_slots
 
-        def scatter(j, lst, src):
-            nc.vector.tensor_copy(planes[j][:].indirect(lst), src)
+        def turn(c_slots, dst):
+            words = c_slots[:].bitcast(F32)
+            for u in range(2):
+                nc.tensor.transpose(dst[:, u, :], words[:, u : H // 2 : 2], ident[:])
 
-        planes = [keep.tile([P, T], F32, name=f"plane{j}") for j in range(2)]
-        rows = [hidden(0), hidden(1)]
-        gather_words(1, PASSES - 1)
-        low0 = keep.tile([P, 2, C], F32, name="low0")
-        high0 = keep.tile([P, 2, C], F32, name="high0")
-        for k in range(2):
-            cols = slice(k * P, (k + 1) * P)
-            turn(rows[k], [(0, 2, low0[:, :, cols]), (2, 4, high0[:, :, cols])])
-            for j in range(2):
-                scatter(j, slots(k, k + 1), low0[:, j, cols])
+        def scatter(u, lst, src):
+            nc.vector.tensor_copy(planes[u][:].indirect(lst), src)
 
-        low1 = keep.tile([P, 2, C], F32, name="low1", tag="low1", align_bytes=64)
-        held = []
-        for k in (2, 3):
-            cols = slice((k - 2) * P, (k - 1) * P)
-            held.append(turn(hidden(k), [(0, 2, low1[:, :, cols])]))
-            planes.append(keep.tile([P, T], F32, name=f"plane{k}", tag=f"act{k}", align_bytes=64))
-            scatter(k, slots(0, 2), high0[:, k - 2, :])
-        w2b = keep.tile([P, N, 4], BF16, name="w2b", tag="gw10", align_bytes=64)
+        for s in range(PASSES):
+            gather_words(0, s)
+            gather_scales(0, s, keep.tile([P, C], U8, name=f"gs0{s}", align_bytes=64))
+        for s in range(PASSES):
+            gather_words(1, s)
+        for s in range(PASSES - 1):
+            gather_scales(1, s, early.tile([P, C], U8, name=f"gs1{s}", offset=s * C, align_bytes=64))
+
+        acc = first_layer(0)
+        rows = [hidden(acc, 0, "c0"), hidden(acc, 1, "c1")]
+        gather_scales(1, PASSES - 1, keep.tile([P, C], U8, name="gs12", tag="act1", align_bytes=64))
+        planes = [keep.tile([P, T], F32, name=f"plane{u}") for u in range(2)]
+        for i in range(2):
+            tr = psum_tr.tile([P, 2, P], F32, name="tr", tag=f"tr{i}")
+            turn(rows[i], tr)
+            pair = keep.tile([P, 2, P], F32, name=f"pair{i}")
+            nc.scalar.copy(pair[:], tr[:])
+            for u in range(2):
+                scatter(u, slots(i, i + 1), pair[:, u, :])
+
+        acc = first_layer(1)
+        rows = [hidden(acc, 2, "c2"), hidden(acc, 3, "c3")]
+        w2b = keep.tile([P, N, 4], BF16, name="w2b", tag="ww01", align_bytes=64)
         for a in range(4):
             cols = slice(a * P, (a + 1) * P)
             nc.scalar.copy(
                 w2b[:, cols, :].rearrange("p (c i) j -> p c j i", i=4),
                 w2raw[:, :, cols].rearrange("p j (c i) -> p c j i", i=4),
             )
-        third = keep.tile([P, C], F32, name="third", tag="w2raw")
-        for i in range(2):
-            nc.scalar.copy(third[:, i * P : (i + 1) * P], held[i][:, 2, :])
-        for j in range(2):
-            scatter(j, slots(2, 4), low1[:, j, :])
-
-        w2q = keep.tile([P, N], U32, name="w2q", tag="low1", align_bytes=64)
-        w2s = keep.tile([P, N], U8, name="w2s", align_bytes=64)
-
-        cb = [keep.tile([P, HALF, 4], BF16, name=f"cb{h}", align_bytes=64) for h in range(2)]
-
-        def interleave(j, h):
-            src = planes[j][:, h * HALF : (h + 1) * HALF]
-            if j >= 2 and h == 0:
-                nc.vector.tensor_copy(cb[h][:, :, j], src)
-            else:
-                nc.scalar.copy(cb[h][:, :, j], src)
-
-        for j in range(2):
-            interleave(j, 0)
-            interleave(j, 1)
+        w2q = keep.tile([P, N], U32, name="w2q", align_bytes=64)
+        w2s = keep.tile([P, N], U8, name="w2s", tag="act3", align_bytes=64)
         nc.vector.quantize_mx(out=w2q[:].bitcast(FP8X4), scales=w2s[:], in_=w2b[:].rearrange("p n j -> p (n j)"))
-        idle = psum_tr.tile([P, N], F32, name="tr")
+        turned = []
+        for i in range(2):
+            tr = psum_tr.tile([P, 2, P], F32, name="tr", tag=f"tr{i}")
+            turn(rows[i], tr)
+            low = keep.tile([P, P], F32, name=f"low{i}", tag=f"low{i}")
+            nc.scalar.copy(low[:], tr[:, 0, :])
+            scatter(0, slots(2 + i, 3 + i), low[:])
+            turned.append(tr)
+        high = keep.tile([P, C], F32, name="high", tag="low0")
+        for i in range(2):
+            nc.scalar.copy(high[:, i * P : (i + 1) * P], turned[i][:, 1, :])
+
+        idle = psum_tr.tile([P, N], F32, name="idle", tag="tr1")
         for r in range(WARM_PASSES):
             nc.tensor.matmul_mx(
                 out=idle[:], lhsT=w2q[:, 0:P].bitcast(FP8X4), lhsT_scale=w2s[:, 0:P],
                 rhs=w2q[:].bitcast(FP8X4), rhs_scale=w2s[:], start=True, stop=True,
             )
-        scatter(2, slots(2, 4), third[:])
-        fourth = keep.tile([P, C], F32, name="fourth", tag="w2raw")
-        for i in range(2):
-            nc.scalar.copy(fourth[:, i * P : (i + 1) * P], held[i][:, 3, :])
-        interleave(2, 1)
-        interleave(2, 0)
-        scatter(3, slots(2, 4), fourth[:])
-        interleave(3, 1)
-        for i in range(2):
-            nc.vector.tensor_copy(cb[0][:, i * P : (i + 1) * P, 3], planes[3][:, i * P : (i + 1) * P])
-        cq = [keep.tile([P, HALF], U32, name=f"cq{h}", align_bytes=64) for h in range(2)]
-        cs = [keep.tile([P, HALF], U8, name=f"cs{h}", align_bytes=64) for h in range(2)]
-        for h, lo, hi in ((0, 0, P), (0, P, HALF), (1, 0, HALF)):
-            nc.vector.quantize_mx(out=cq[h][:, lo:hi].bitcast(FP8X4), scales=cs[h][:, lo:hi], in_=cb[h][:, lo:hi, :].rearrange("p t j -> p (t j)"))
-        for h in range(2):
-            for a in range(4):
-                res = psum_tr.tile([P, HALF], F32, name="tr") if 4 * h + a >= 3 else psum_acc.tile([P, HALF], F32, name="acc")
+        bounds = (0, P, HALF, T)
+        cb = [keep.tile([P, bounds[g + 1] - bounds[g], 2], F32, name=f"cb{g}", align_bytes=64) for g in range(3)]
+        for g in range(3):
+            nc.scalar.copy(cb[g][:, :, 0], planes[0][:, bounds[g] : bounds[g + 1]])
+        scatter(1, slots(2, 4), high[:])
+        for g in range(2):
+            nc.vector.tensor_copy(cb[g][:, :, 1], planes[1][:, bounds[g] : bounds[g + 1]])
+        nc.scalar.copy(cb[2][:, :, 1], planes[1][:, HALF:])
+        cq = [keep.tile([P, bounds[g + 1] - bounds[g]], U32, name=f"cq{g}", align_bytes=64) for g in range(3)]
+        cs = [keep.tile([P, bounds[g + 1] - bounds[g]], U8, name=f"cs{g}", align_bytes=64) for g in range(3)]
+        for g in range(3):
+            nc.vector.quantize_mx(out=cq[g][:].bitcast(FP8X4), scales=cs[g][:], in_=cb[g][:].rearrange("p t u -> p (t u)").bitcast(BF16))
+        rows_out = out.rearrange("(a p) t -> p a t", p=P)
+        pieces = [(g, a, a + 2) for g in range(2) for a in (0, 2)] + [(2, a, a + 1) for a in range(4)]
+        for n, (g, lo, hi) in enumerate(pieces):
+            width = bounds[g + 1] - bounds[g]
+            if n >= 6:
+                res = psum_tr.tile([P, hi - lo, width], F32, name="res", tag=f"tr{n - 6}")
+            else:
+                res = psum_acc.tile([P, hi - lo, width], F32, name="acc")
+            for a in range(lo, hi):
                 cols = slice(a * P, (a + 1) * P)
                 nc.tensor.matmul_mx(
-                    out=res[:],
+                    out=res[:, a - lo, :],
                     lhsT=w2q[:, cols].bitcast(FP8X4),
                     lhsT_scale=w2s[:, cols],
-                    rhs=cq[h][:].bitcast(FP8X4),
-                    rhs_scale=cs[h][:],
+                    rhs=cq[g][:].bitcast(FP8X4),
+                    rhs_scale=cs[g][:],
                     start=True,
                     stop=True,
                 )
-                staged = keep.tile([P, HALF], F32, name=f"staged{h}{a}")
-                if a % 2 == 0:
-                    nc.scalar.copy(staged[:], res[:])
-                else:
-                    nc.vector.tensor_copy(staged[:], res[:])
-                nc.sync.dma_start(out[cols, h * HALF : (h + 1) * HALF], staged[:])
+            staged = keep.tile([P, hi - lo, width], F32, name=f"staged{n}")
+            if n % 2 == 0:
+                nc.scalar.copy(staged[:], res[:])
+            else:
+                nc.vector.tensor_copy(staged[:], res[:])
+            nc.sync.dma_start(rows_out[:, lo:hi, bounds[g] : bounds[g + 1]], staged[:])

@@ -29,6 +29,7 @@ def tile_moe_sdn_glu_gelu_kernel(tc, x_words, x_scales, w1_words, w1_scales, w3_
     with ExitStack() as ctx:
         keep = ctx.enter_context(tc.tile_pool(name="keep", bufs=1))
         early = ctx.enter_context(tc.tile_pool(name="early", bufs=1))
+        late = ctx.enter_context(tc.tile_pool(name="late", bufs=1))
         psum_acc = ctx.enter_context(tc.psum_pool(name="psum_acc", bufs=6))
         psum_tr = ctx.enter_context(tc.psum_pool(name="psum_tr", bufs=1))
 
@@ -55,25 +56,33 @@ def tile_moe_sdn_glu_gelu_kernel(tc, x_words, x_scales, w1_words, w1_scales, w3_
                 x_words[lo:hi].rearrange("s p t d -> p s (t d)").bitcast(I32),
             )
 
-        def load_matrix(m, e):
-            words, scales = ((w1_words, w1_scales), (w3_words, w3_scales))[m]
-            nc.sync.dma_start(ww[m][e][:].bitcast(I32), words[e].rearrange("s p b -> p s b").bitcast(I32))
+        def load_words(m, e):
+            nc.sync.dma_start(ww[m][e][:].bitcast(I32), (w1_words, w3_words)[m][e].rearrange("s p b -> p s b").bitcast(I32))
+
+        def load_scales(m, e):
             for r in range(4):
-                nc.sync.dma_start(ws[m][e][r:P:32].bitcast(I32), scales[e, :, r:16:4, :].rearrange("s q i -> q s i").bitcast(I32))
+                nc.sync.dma_start(ws[m][e][r:P:32].bitcast(I32), (w1_scales, w3_scales)[m][e, :, r:16:4, :].rearrange("s q i -> q s i").bitcast(I32))
 
         nc.sync.dma_start(offsets[:], offs)
         load_tokens(0, 1)
         for r in range(4):
             nc.sync.dma_start(xs[r:P:32].bitcast(I32).rearrange("q (s t) -> q s t", s=PASSES), x_scales[:, r:16:4, :].rearrange("s q t -> q s t").bitcast(I32))
-        load_tokens(1, PASSES)
-        load_matrix(0, 0)
-        load_matrix(1, 0)
-        load_matrix(0, 1)
+        load_words(0, 0)
+        load_tokens(1, 2)
+        load_scales(0, 0)
+        load_tokens(2, 3)
+        load_words(1, 0)
+        load_scales(1, 0)
+        load_words(0, 1)
+        load_scales(0, 1)
         with nc.allow_non_contiguous_dma(reason="one gate value a partition"):
             nc.sync.dma_start(gcol[:], gate[0:1, :].rearrange("o (k p) -> p (o k)", p=P))
-        w2raw = keep.tile([P, 4, N], F32, name="w2raw")
-        nc.sync.dma_start(w2raw[:], w2.rearrange("(p j) n -> p j n", j=4))
-        load_matrix(1, 1)
+        w2raw = [late.tile([P, 4, N // 2], F32, name=f"w2raw{b}", offset=8 * N * (1 - b)) for b in range(2)]
+        w2rows = w2.rearrange("(p j) n -> p j n", j=4)
+        nc.sync.dma_start(w2raw[0][:], w2rows[:, :, : N // 2])
+        load_words(1, 1)
+        load_scales(1, 1)
+        nc.sync.dma_start(w2raw[1][:], w2rows[:, :, N // 2 :])
 
         gw = {}
         gs = {}
@@ -92,18 +101,17 @@ def tile_moe_sdn_glu_gelu_kernel(tc, x_words, x_scales, w1_words, w1_scales, w3_
 
         def first_layer(e):
             acc = {(k, m): psum_acc.tile([P, H], F32, name="acc") for m in range(2) for k in range(2)}
-            for m in range(2):
-                for s in range(PASSES):
-                    for k in range(2):
-                        nc.tensor.matmul_mx(
-                            out=acc[k, m][:],
-                            lhsT=gw[e, s][:, k * P : (k + 1) * P].bitcast(FP8X4),
-                            lhsT_scale=gs[e, s][:, k * P : (k + 1) * P],
-                            rhs=ww[m][e][:, s, :].bitcast(FP4X4),
-                            rhs_scale=ws[m][e][:, s, :],
-                            start=(s == 0),
-                            stop=(s == PASSES - 1),
-                        )
+            order = [(0, s, k) for s in range(PASSES) for k in range(2)] + [(1, s, k) for k in range(2) for s in range(PASSES)]
+            for m, s, k in order:
+                nc.tensor.matmul_mx(
+                    out=acc[k, m][:],
+                    lhsT=gw[e, s][:, k * P : (k + 1) * P].bitcast(FP8X4),
+                    lhsT_scale=gs[e, s][:, k * P : (k + 1) * P],
+                    rhs=ww[m][e][:, s, :].bitcast(FP4X4),
+                    rhs_scale=ws[m][e][:, s, :],
+                    start=(s == 0),
+                    stop=(s == PASSES - 1),
+                )
             return acc
 
         def hidden(acc, k, tag):
@@ -148,7 +156,7 @@ def tile_moe_sdn_glu_gelu_kernel(tc, x_words, x_scales, w1_words, w1_scales, w3_
             cols = slice(a * P, (a + 1) * P)
             nc.scalar.copy(
                 w2b[:, cols, :].rearrange("p (c i) j -> p c j i", i=4),
-                w2raw[:, :, cols].rearrange("p j (c i) -> p c j i", i=4),
+                w2raw[a // 2][:, :, a % 2 * P : (a % 2 + 1) * P].rearrange("p j (c i) -> p c j i", i=4),
             )
         w2q = keep.tile([P, N], U32, name="w2q", align_bytes=64)
         w2s = keep.tile([P, N], U8, name="w2s", tag="act3", align_bytes=64)
@@ -157,11 +165,11 @@ def tile_moe_sdn_glu_gelu_kernel(tc, x_words, x_scales, w1_words, w1_scales, w3_
         for i in range(2):
             tr = psum_tr.tile([P, 2, P], F32, name="tr", tag=f"tr{i}")
             turn(rows[i], tr)
-            low = keep.tile([P, P], F32, name=f"low{i}", tag=f"low{i}")
+            low = late.tile([P, P], F32, name=f"low{i}", offset=4 * C * i)
             nc.scalar.copy(low[:], tr[:, 0, :])
             scatter(0, slots(2 + i, 3 + i), low[:])
             turned.append(tr)
-        high = keep.tile([P, C], F32, name="high", tag="low0")
+        high = late.tile([P, C], F32, name="high", offset=0)
         for i in range(2):
             nc.scalar.copy(high[:, i * P : (i + 1) * P], turned[i][:, 1, :])
 
@@ -171,40 +179,35 @@ def tile_moe_sdn_glu_gelu_kernel(tc, x_words, x_scales, w1_words, w1_scales, w3_
                 out=idle[:], lhsT=w2q[:, 0:P].bitcast(FP8X4), lhsT_scale=w2s[:, 0:P],
                 rhs=w2q[:].bitcast(FP8X4), rhs_scale=w2s[:], start=True, stop=True,
             )
-        bounds = (0, P, HALF, T)
-        cb = [keep.tile([P, bounds[g + 1] - bounds[g], 2], F32, name=f"cb{g}", align_bytes=64) for g in range(3)]
-        for g in range(3):
-            nc.scalar.copy(cb[g][:, :, 0], planes[0][:, bounds[g] : bounds[g + 1]])
+        cb = [keep.tile([P, HALF, 2], F32, name=f"cb{h}", align_bytes=64) for h in range(2)]
+        for h in range(2):
+            nc.scalar.copy(cb[h][:, :, 0], planes[0][:, h * HALF : (h + 1) * HALF])
         scatter(1, slots(2, 4), high[:])
-        for g in range(2):
-            nc.vector.tensor_copy(cb[g][:, :, 1], planes[1][:, bounds[g] : bounds[g + 1]])
-        nc.scalar.copy(cb[2][:, :, 1], planes[1][:, HALF:])
-        cq = [keep.tile([P, bounds[g + 1] - bounds[g]], U32, name=f"cq{g}", align_bytes=64) for g in range(3)]
-        cs = [keep.tile([P, bounds[g + 1] - bounds[g]], U8, name=f"cs{g}", align_bytes=64) for g in range(3)]
-        for g in range(3):
-            nc.vector.quantize_mx(out=cq[g][:].bitcast(FP8X4), scales=cs[g][:], in_=cb[g][:].rearrange("p t u -> p (t u)").bitcast(BF16))
-        rows_out = out.rearrange("(a p) t -> p a t", p=P)
-        pieces = [(g, a, a + 2) for g in range(2) for a in (0, 2)] + [(2, a, a + 1) for a in range(4)]
-        for n, (g, lo, hi) in enumerate(pieces):
-            width = bounds[g + 1] - bounds[g]
-            if n >= 6:
-                res = psum_tr.tile([P, hi - lo, width], F32, name="res", tag=f"tr{n - 6}")
-            else:
-                res = psum_acc.tile([P, hi - lo, width], F32, name="acc")
-            for a in range(lo, hi):
+        nc.vector.tensor_copy(cb[0][:, :, 1], planes[1][:, :HALF])
+        nc.scalar.copy(cb[1][:, :, 1], planes[1][:, HALF:])
+        cq = [keep.tile([P, HALF], U32, name=f"cq{h}", align_bytes=64) for h in range(2)]
+        cs = [keep.tile([P, HALF], U8, name=f"cs{h}", align_bytes=64) for h in range(2)]
+        for h in range(2):
+            nc.vector.quantize_mx(out=cq[h][:].bitcast(FP8X4), scales=cs[h][:], in_=cb[h][:].rearrange("p t u -> p (t u)").bitcast(BF16))
+        for h in range(2):
+            for a in range(4):
+                if h == 1 and a >= 2:
+                    res = psum_tr.tile([P, HALF], F32, name="res", tag=f"tr{a - 2}")
+                else:
+                    res = psum_acc.tile([P, HALF], F32, name="acc")
                 cols = slice(a * P, (a + 1) * P)
                 nc.tensor.matmul_mx(
-                    out=res[:, a - lo, :],
+                    out=res[:],
                     lhsT=w2q[:, cols].bitcast(FP8X4),
                     lhsT_scale=w2s[:, cols],
-                    rhs=cq[g][:].bitcast(FP8X4),
-                    rhs_scale=cs[g][:],
+                    rhs=cq[h][:].bitcast(FP8X4),
+                    rhs_scale=cs[h][:],
                     start=True,
                     stop=True,
                 )
-            staged = keep.tile([P, hi - lo, width], F32, name=f"staged{n}")
-            if n % 2 == 0:
-                nc.scalar.copy(staged[:], res[:])
-            else:
-                nc.vector.tensor_copy(staged[:], res[:])
-            nc.sync.dma_start(rows_out[:, lo:hi, bounds[g] : bounds[g + 1]], staged[:])
+                staged = keep.tile([P, HALF], F32, name=f"staged{h}{a}")
+                if a % 2 == 0:
+                    nc.scalar.copy(staged[:], res[:])
+                else:
+                    nc.vector.tensor_copy(staged[:], res[:])
+                nc.sync.dma_start(out[cols, h * HALF : (h + 1) * HALF], staged[:])

@@ -21,6 +21,7 @@ P = 128
 PASSES = K // 512
 TILES = E * C // P
 HALF = T // 2
+WORDS = PASSES * 2 * H
 WARM_PASSES = 4
 
 
@@ -30,6 +31,7 @@ def tile_moe_sdn_glu_gelu_kernel(tc, x_words, x_scales, w1_words, w1_scales, w3_
         keep = ctx.enter_context(tc.tile_pool(name="keep", bufs=1))
         early = ctx.enter_context(tc.tile_pool(name="early", bufs=1))
         late = ctx.enter_context(tc.tile_pool(name="late", bufs=1))
+        words = ctx.enter_context(tc.tile_pool(name="words", bufs=1))
         psum_acc = ctx.enter_context(tc.psum_pool(name="psum_acc", bufs=6))
         psum_tr = ctx.enter_context(tc.psum_pool(name="psum_tr", bufs=1))
 
@@ -37,17 +39,14 @@ def tile_moe_sdn_glu_gelu_kernel(tc, x_words, x_scales, w1_words, w1_scales, w3_
         xw = early.tile([P, PASSES * T], I32, name="xw", offset=0, align_bytes=64)
         xs = keep.tile([P, PASSES * T], U8, name="xs", align_bytes=64)
         ws = [[keep.tile([P, PASSES, H], U8, name=f"ws{m}{e}", align_bytes=64) for e in range(E)] for m in range(2)]
-        ww = [[keep.tile([P, PASSES, 2 * H], U8, name=f"ww{m}{e}", tag=f"ww{m}{e}", align_bytes=64) for e in range(E)] for m in range(2)]
+        ww = [[words.tile([P, PASSES, 2 * H], U8, name=f"ww{m}{e}", offset=(m * E + e) * WORDS, align_bytes=64) for e in range(E)] for m in range(2)]
         gcol = keep.tile([P, TILES], F32, name="gcol")
         ident = keep.tile([P, P], F32, name="ident")
-        warm = [keep.tile([P, 1], F32, name=f"warm{m}") for m in range(2)]
 
         nc.gpsimd.memset(xs[:].bitcast(I32), 0)
         for e in range(E):
             for m in range(2):
                 nc.vector.memset(ws[m][e][:].bitcast(I32), 0)
-        nc.gpsimd.memset(warm[0][:], 0.0)
-        nc.scalar.activation(warm[1][:], warm[0][:], GELU)
         make_identity(nc, ident[:])
 
         def load_tokens(lo, hi):
@@ -59,12 +58,12 @@ def tile_moe_sdn_glu_gelu_kernel(tc, x_words, x_scales, w1_words, w1_scales, w3_
         def load_words(m, e):
             nc.sync.dma_start(ww[m][e][:].bitcast(I32), (w1_words, w3_words)[m][e].rearrange("s p b -> p s b").bitcast(I32))
 
-        def load_scales(m, e):
-            for r in range(4):
+        def load_scales(m, e, rows=range(4)):
+            for r in rows:
                 nc.sync.dma_start(ws[m][e][r:P:32].bitcast(I32), (w1_scales, w3_scales)[m][e, :, r:16:4, :].rearrange("s q i -> q s i").bitcast(I32))
 
-        nc.sync.dma_start(offsets[:], offs)
         load_tokens(0, 1)
+        nc.sync.dma_start(offsets[:], offs)
         for r in range(4):
             nc.sync.dma_start(xs[r:P:32].bitcast(I32).rearrange("q (s t) -> q s t", s=PASSES), x_scales[:, r:16:4, :].rearrange("s q t -> q s t").bitcast(I32))
         load_words(0, 0)
@@ -74,11 +73,12 @@ def tile_moe_sdn_glu_gelu_kernel(tc, x_words, x_scales, w1_words, w1_scales, w3_
         load_words(1, 0)
         load_scales(1, 0)
         load_words(0, 1)
-        load_scales(0, 1)
+        load_scales(0, 1, range(3))
         with nc.allow_non_contiguous_dma(reason="one gate value a partition"):
             nc.sync.dma_start(gcol[:], gate[0:1, :].rearrange("o (k p) -> p (o k)", p=P))
-        w2raw = [late.tile([P, 4, N // 2], F32, name=f"w2raw{b}", offset=8 * N * (1 - b)) for b in range(2)]
+        load_scales(0, 1, range(3, 4))
         w2rows = w2.rearrange("(p j) n -> p j n", j=4)
+        w2raw = [late.tile([P, 4, N // 2], F32, name=f"w2raw{b}", offset=8 * N * (1 - b), align_bytes=64) for b in range(2)]
         nc.sync.dma_start(w2raw[0][:], w2rows[:, :, : N // 2])
         load_words(1, 1)
         load_scales(1, 1)
@@ -139,56 +139,72 @@ def tile_moe_sdn_glu_gelu_kernel(tc, x_words, x_scales, w1_words, w1_scales, w3_
 
         acc = first_layer(0)
         rows = [hidden(acc, 0, "c0"), hidden(acc, 1, "c1")]
-        gather_scales(1, PASSES - 1, keep.tile([P, C], U8, name="gs12", tag="act1", align_bytes=64))
         planes = [keep.tile([P, T], F32, name=f"plane{u}") for u in range(2)]
+        low = keep.tile([P, C], F32, name="low0")
+        high = keep.tile([P, P], F32, name="high0")
+        turned = [psum_tr.tile([P, 2, P], F32, name="tr", tag=f"tr{i}") for i in range(2)]
         for i in range(2):
-            tr = psum_tr.tile([P, 2, P], F32, name="tr", tag=f"tr{i}")
-            turn(rows[i], tr)
-            pair = keep.tile([P, 2, P], F32, name=f"pair{i}")
-            nc.scalar.copy(pair[:], tr[:])
-            for u in range(2):
-                scatter(u, slots(i, i + 1), pair[:, u, :])
+            turn(rows[i], turned[i])
+        gather_scales(1, PASSES - 1, keep.tile([P, C], U8, name="gs12", tag="act0", align_bytes=64))
+        nc.scalar.copy(high[:], turned[0][:, 1, :])
+        scatter(1, slots(0, 1), high[:])
+        for i in range(2):
+            nc.scalar.copy(low[:, i * P : (i + 1) * P], turned[i][:, 0, :])
+        scatter(0, slots(0, 2), low[:])
 
         acc = first_layer(1)
         rows = [hidden(acc, 2, "c2"), hidden(acc, 3, "c3")]
-        w2b = keep.tile([P, N, 4], BF16, name="w2b", tag="ww01", align_bytes=64)
-        for a in range(4):
-            cols = slice(a * P, (a + 1) * P)
-            nc.scalar.copy(
-                w2b[:, cols, :].rearrange("p (c i) j -> p c j i", i=4),
-                w2raw[a // 2][:, :, a % 2 * P : (a % 2 + 1) * P].rearrange("p j (c i) -> p c j i", i=4),
-            )
-        w2q = keep.tile([P, N], U32, name="w2q", align_bytes=64)
-        w2s = keep.tile([P, N], U8, name="w2s", tag="act3", align_bytes=64)
-        nc.vector.quantize_mx(out=w2q[:].bitcast(FP8X4), scales=w2s[:], in_=w2b[:].rearrange("p n j -> p (n j)"))
-        turned = []
+
+        def cast_w2(b):
+            w2b = keep.tile([P, N // 2, 4], BF16, name=f"w2b{b}", tag=f"w2b{b}", align_bytes=64)
+            for c in range(0, N // 2, P):
+                nc.scalar.copy(
+                    w2b[:, c : c + P, :].rearrange("p (c i) j -> p c j i", i=4),
+                    w2raw[b][:, :, c : c + P].rearrange("p j (c i) -> p c j i", i=4),
+                )
+            return w2b
+
+        def quantise_w2(b, w2b, scales):
+            w2q.append(keep.tile([P, N // 2], U32, name=f"w2q{b}", align_bytes=64))
+            w2s.append(scales)
+            nc.vector.quantize_mx(out=w2q[b][:].bitcast(FP8X4), scales=w2s[b][:], in_=w2b[:].rearrange("p n j -> p (n j)"))
+
+        w2q = []
+        w2s = []
+        held = words.tile([P, P], F32, name="held", offset=3 * WORDS, align_bytes=64)
+        nc.scalar.copy(held[:], turned[1][:, 1, :])
+        w2b = [cast_w2(b) for b in range(2)]
+        quantise_w2(0, w2b[0], words.tile([P, N // 2], U8, name="w2s0", offset=3 * WORDS + 4 * P, align_bytes=64))
+        scatter(1, slots(1, 2), held[:])
+        turned = [psum_tr.tile([P, 2, P], F32, name="tr", tag=f"tr{i}") for i in range(2)]
+        low = late.tile([P, C], F32, name="low1", offset=0, align_bytes=64)
         for i in range(2):
-            tr = psum_tr.tile([P, 2, P], F32, name="tr", tag=f"tr{i}")
-            turn(rows[i], tr)
-            low = late.tile([P, P], F32, name=f"low{i}", offset=4 * C * i)
-            nc.scalar.copy(low[:], tr[:, 0, :])
-            scatter(0, slots(2 + i, 3 + i), low[:])
-            turned.append(tr)
-        high = late.tile([P, C], F32, name="high", offset=0)
+            turn(rows[i], turned[i])
+            nc.scalar.copy(low[:, i * P : (i + 1) * P], turned[i][:, 0, :])
+        scatter(0, slots(2, 3), low[:, :P])
+        quantise_w2(1, w2b[1], keep.tile([P, N // 2], U8, name="w2s1", tag="c3", align_bytes=64))
+        scatter(0, slots(3, 4), low[:, P:])
+        high = keep.tile([P, C], F32, name="high1", tag="w2b1", align_bytes=64)
         for i in range(2):
             nc.scalar.copy(high[:, i * P : (i + 1) * P], turned[i][:, 1, :])
 
-        idle = psum_tr.tile([P, N], F32, name="idle", tag="tr1")
+        idle = psum_tr.tile([P, H], F32, name="idle", tag="tr1")
         for r in range(WARM_PASSES):
             nc.tensor.matmul_mx(
-                out=idle[:], lhsT=w2q[:, 0:P].bitcast(FP8X4), lhsT_scale=w2s[:, 0:P],
-                rhs=w2q[:].bitcast(FP8X4), rhs_scale=w2s[:], start=True, stop=True,
+                out=idle[:], lhsT=w2q[1][:, 0:P].bitcast(FP8X4), lhsT_scale=w2s[1][:, 0:P],
+                rhs=ww[0][1][:, 0, :].bitcast(FP4X4), rhs_scale=ws[0][1][:, 0, :], start=True, stop=True,
             )
         cb = [keep.tile([P, HALF, 2], F32, name=f"cb{h}", align_bytes=64) for h in range(2)]
         for h in range(2):
             nc.scalar.copy(cb[h][:, :, 0], planes[0][:, h * HALF : (h + 1) * HALF])
         scatter(1, slots(2, 4), high[:])
-        nc.vector.tensor_copy(cb[0][:, :, 1], planes[1][:, :HALF])
+        for lo in (0, P):
+            nc.vector.tensor_copy(cb[0][:, lo : lo + P, 1], planes[1][:, lo : lo + P])
         nc.scalar.copy(cb[1][:, :, 1], planes[1][:, HALF:])
         cq = [keep.tile([P, HALF], U32, name=f"cq{h}", align_bytes=64) for h in range(2)]
         cs = [keep.tile([P, HALF], U8, name=f"cs{h}", align_bytes=64) for h in range(2)]
-        for h in range(2):
-            nc.vector.quantize_mx(out=cq[h][:].bitcast(FP8X4), scales=cs[h][:], in_=cb[h][:].rearrange("p t u -> p (t u)").bitcast(BF16))
+        for h, lo, hi in ((0, 0, P), (0, P, HALF), (1, 0, HALF)):
+            nc.vector.quantize_mx(out=cq[h][:, lo:hi].bitcast(FP8X4), scales=cs[h][:, lo:hi], in_=cb[h][:, lo:hi, :].rearrange("p t u -> p (t u)").bitcast(BF16))
         for h in range(2):
             for a in range(4):
                 if h == 1 and a >= 2:
@@ -196,10 +212,11 @@ def tile_moe_sdn_glu_gelu_kernel(tc, x_words, x_scales, w1_words, w1_scales, w3_
                 else:
                     res = psum_acc.tile([P, HALF], F32, name="acc")
                 cols = slice(a * P, (a + 1) * P)
+                part = slice(a % 2 * P, (a % 2 + 1) * P)
                 nc.tensor.matmul_mx(
                     out=res[:],
-                    lhsT=w2q[:, cols].bitcast(FP8X4),
-                    lhsT_scale=w2s[:, cols],
+                    lhsT=w2q[a // 2][:, part].bitcast(FP8X4),
+                    lhsT_scale=w2s[a // 2][:, part],
                     rhs=cq[h][:].bitcast(FP8X4),
                     rhs_scale=cs[h][:],
                     start=True,

@@ -174,7 +174,6 @@ def tile_moe_sdn_glu_gelu_kernel(tc, x_words, x_scales, w1_words, w1_scales, w3_
         held = words.tile([P, P], F32, name="held", offset=3 * WORDS, align_bytes=64)
         nc.scalar.copy(held[:], turned[1][:, 1, :])
         w2b = [cast_w2(b) for b in range(2)]
-        quantise_w2(0, w2b[0], words.tile([P, N // 2], U8, name="w2s0", offset=3 * WORDS + 4 * P, align_bytes=64))
         scatter(1, slots(1, 2), held[:])
         turned = [psum_tr.tile([P, 2, P], F32, name="tr", tag=f"tr{i}") for i in range(2)]
         low = late.tile([P, C], F32, name="low1", offset=0, align_bytes=64)
@@ -182,16 +181,16 @@ def tile_moe_sdn_glu_gelu_kernel(tc, x_words, x_scales, w1_words, w1_scales, w3_
             turn(rows[i], turned[i])
             nc.scalar.copy(low[:, i * P : (i + 1) * P], turned[i][:, 0, :])
         scatter(0, slots(2, 3), low[:, :P])
-        quantise_w2(1, w2b[1], keep.tile([P, N // 2], U8, name="w2s1", tag="c3", align_bytes=64))
+        quantise_w2(0, w2b[0], keep.tile([P, N // 2], U8, name="w2s0", tag="c3", align_bytes=64))
         scatter(0, slots(3, 4), low[:, P:])
-        high = keep.tile([P, C], F32, name="high1", tag="w2b1", align_bytes=64)
+        high = keep.tile([P, C], F32, name="high1", tag="w2b0", align_bytes=64)
         for i in range(2):
             nc.scalar.copy(high[:, i * P : (i + 1) * P], turned[i][:, 1, :])
 
         idle = psum_tr.tile([P, H], F32, name="idle", tag="tr1")
         for r in range(WARM_PASSES):
             nc.tensor.matmul_mx(
-                out=idle[:], lhsT=w2q[1][:, 0:P].bitcast(FP8X4), lhsT_scale=w2s[1][:, 0:P],
+                out=idle[:], lhsT=w2q[0][:, 0:P].bitcast(FP8X4), lhsT_scale=w2s[0][:, 0:P],
                 rhs=ww[0][1][:, 0, :].bitcast(FP4X4), rhs_scale=ws[0][1][:, 0, :], start=True, stop=True,
             )
         cb = [keep.tile([P, HALF, 2], F32, name=f"cb{h}", align_bytes=64) for h in range(2)]
@@ -203,28 +202,36 @@ def tile_moe_sdn_glu_gelu_kernel(tc, x_words, x_scales, w1_words, w1_scales, w3_
         nc.scalar.copy(cb[1][:, :, 1], planes[1][:, HALF:])
         cq = [keep.tile([P, HALF], U32, name=f"cq{h}", align_bytes=64) for h in range(2)]
         cs = [keep.tile([P, HALF], U8, name=f"cs{h}", align_bytes=64) for h in range(2)]
-        for h, lo, hi in ((0, 0, P), (0, P, HALF), (1, 0, HALF)):
+
+        def quantise_c(h, lo, hi):
             nc.vector.quantize_mx(out=cq[h][:, lo:hi].bitcast(FP8X4), scales=cs[h][:, lo:hi], in_=cb[h][:, lo:hi, :].rearrange("p t u -> p (t u)").bitcast(BF16))
-        for h in range(2):
-            for a in range(4):
-                if h == 1 and a >= 2:
-                    res = psum_tr.tile([P, HALF], F32, name="res", tag=f"tr{a - 2}")
-                else:
-                    res = psum_acc.tile([P, HALF], F32, name="acc")
-                cols = slice(a * P, (a + 1) * P)
-                part = slice(a % 2 * P, (a % 2 + 1) * P)
-                nc.tensor.matmul_mx(
-                    out=res[:],
-                    lhsT=w2q[a // 2][:, part].bitcast(FP8X4),
-                    lhsT_scale=w2s[a // 2][:, part],
-                    rhs=cq[h][:].bitcast(FP8X4),
-                    rhs_scale=cs[h][:],
-                    start=True,
-                    stop=True,
-                )
-                staged = keep.tile([P, HALF], F32, name=f"staged{h}{a}")
-                if a % 2 == 0:
-                    nc.scalar.copy(staged[:], res[:])
-                else:
-                    nc.vector.tensor_copy(staged[:], res[:])
-                nc.sync.dma_start(out[cols, h * HALF : (h + 1) * HALF], staged[:])
+
+        quantise_c(0, 0, P)
+        quantise_c(0, P, HALF)
+        quantise_w2(1, w2b[1], keep.tile([P, N // 2], U8, name="w2s1", tag="w2b0", align_bytes=64))
+        quantise_c(1, 0, HALF)
+        pieces = [(0, 0, P), (1, 0, P), (2, 0, HALF), (3, 0, HALF), (0, P, T), (1, P, T), (2, HALF, T), (3, HALF, T)]
+        for j, (a, lo, hi) in enumerate(pieces):
+            if j >= 6:
+                res = psum_tr.tile([P, hi - lo], F32, name="res", tag=f"tr{j - 6}")
+            else:
+                res = psum_acc.tile([P, hi - lo], F32, name="acc")
+            part = slice(a % 2 * P, (a % 2 + 1) * P)
+            for h in range(2):
+                first, last = max(lo, h * HALF), min(hi, (h + 1) * HALF)
+                if first < last:
+                    nc.tensor.matmul_mx(
+                        out=res[:, first - lo : last - lo],
+                        lhsT=w2q[a // 2][:, part].bitcast(FP8X4),
+                        lhsT_scale=w2s[a // 2][:, part],
+                        rhs=cq[h][:, first - h * HALF : last - h * HALF].bitcast(FP8X4),
+                        rhs_scale=cs[h][:, first - h * HALF : last - h * HALF],
+                        start=True,
+                        stop=True,
+                    )
+            staged = keep.tile([P, hi - lo], F32, name=f"staged{j}")
+            if j % 2 == 0:
+                nc.scalar.copy(staged[:], res[:])
+            else:
+                nc.vector.tensor_copy(staged[:], res[:])
+            nc.sync.dma_start(out[a * P : (a + 1) * P, lo:hi], staged[:])

@@ -32,14 +32,14 @@ def tile_moe_sdn_glu_gelu_kernel(tc, x_words, x_scales, w1_words, w1_scales, w3_
         early = ctx.enter_context(tc.tile_pool(name="early", bufs=1))
         late = ctx.enter_context(tc.tile_pool(name="late", bufs=1))
         words = ctx.enter_context(tc.tile_pool(name="words", bufs=1))
-        psum_acc = ctx.enter_context(tc.psum_pool(name="psum_acc", bufs=6))
-        psum_tr = ctx.enter_context(tc.psum_pool(name="psum_tr", bufs=1))
+        psum = ctx.enter_context(tc.psum_pool(name="psum", bufs=1))
 
         offsets = keep.tile([P, T // 16], U16, name="offsets")
-        xw = early.tile([P, PASSES * T], I32, name="xw", offset=0, align_bytes=64)
-        xs = keep.tile([P, PASSES * T], U8, name="xs", align_bytes=64)
+        xw = keep.tile([P, PASSES * T], I32, name="xw", align_bytes=64)
+        xs = early.tile([P, PASSES * T], U8, name="xs", offset=0, align_bytes=64)
         ws = [[keep.tile([P, PASSES, H], U8, name=f"ws{m}{e}", align_bytes=64) for e in range(E)] for m in range(2)]
         ww = [[words.tile([P, PASSES, 2 * H], U8, name=f"ww{m}{e}", offset=(m * E + e) * WORDS, align_bytes=64) for e in range(E)] for m in range(2)]
+        moved_scales = keep.tile([P, 2, C], U8, name="moved_scales", align_bytes=64)
         gcol = keep.tile([P, TILES], F32, name="gcol")
         ident = keep.tile([P, P], F32, name="ident")
 
@@ -47,6 +47,7 @@ def tile_moe_sdn_glu_gelu_kernel(tc, x_words, x_scales, w1_words, w1_scales, w3_
         for e in range(E):
             for m in range(2):
                 nc.vector.memset(ws[m][e][:].bitcast(I32), 0)
+        nc.vector.memset(moved_scales[:].bitcast(I32), 0)
         make_identity(nc, ident[:])
 
         def load_tokens(lo, hi):
@@ -67,22 +68,11 @@ def tile_moe_sdn_glu_gelu_kernel(tc, x_words, x_scales, w1_words, w1_scales, w3_
         for r in range(4):
             nc.sync.dma_start(xs[r:P:32].bitcast(I32).rearrange("q (s t) -> q s t", s=PASSES), x_scales[:, r:16:4, :].rearrange("s q t -> q s t").bitcast(I32))
         load_words(0, 0)
-        load_tokens(1, 2)
         load_scales(0, 0)
+        load_tokens(1, 2)
         load_tokens(2, 3)
         load_words(1, 0)
         load_scales(1, 0)
-        load_words(0, 1)
-        load_scales(0, 1, range(3))
-        with nc.allow_non_contiguous_dma(reason="one gate value a partition"):
-            nc.sync.dma_start(gcol[:], gate[0:1, :].rearrange("o (k p) -> p (o k)", p=P))
-        load_scales(0, 1, range(3, 4))
-        w2rows = w2.rearrange("(p j) n -> p j n", j=4)
-        w2raw = [late.tile([P, 4, N // 2], F32, name=f"w2raw{b}", offset=8 * N * (1 - b), align_bytes=64) for b in range(2)]
-        nc.sync.dma_start(w2raw[0][:], w2rows[:, :, : N // 2])
-        load_words(1, 1)
-        load_scales(1, 1)
-        nc.sync.dma_start(w2raw[1][:], w2rows[:, :, N // 2 :])
 
         gw = {}
         gs = {}
@@ -90,18 +80,22 @@ def tile_moe_sdn_glu_gelu_kernel(tc, x_words, x_scales, w1_words, w1_scales, w3_
         def slots(lo, hi):
             return offsets[:, lo * P // 16 : hi * P // 16]
 
+        def bank(j, width):
+            return psum.tile([P, width], F32, name=f"bank{j}", tag=f"bank{j}")
+
         def gather_words(e, s):
-            end = (s + 1) * T if e == 0 or s == PASSES - 1 else PASSES * T
-            gw[e, s] = keep.tile([P, C], U32, name=f"gw{e}{s}", align_bytes=64)
+            end = (s + 1) * T if e == 0 else PASSES * T
+            if (e, s) == (1, PASSES - 1):
+                gw[e, s] = early.tile([P, C], U32, name="gw_last", offset=0, align_bytes=64)
+            else:
+                gw[e, s] = keep.tile([P, C], U32, name=f"gw{e}{s}", align_bytes=64)
             nc.vector.tensor_copy(gw[e, s][:], xw[:, s * T : end].bitcast(U32).indirect(slots(2 * e, 2 * e + 2)))
 
         def gather_scales(e, s, dst):
             gs[e, s] = dst
             nc.vector.tensor_copy(dst[:], xs[:, s * T : (s + 1) * T].indirect(slots(2 * e, 2 * e + 2)))
 
-        def first_layer(e):
-            acc = {(k, m): psum_acc.tile([P, H], F32, name="acc") for m in range(2) for k in range(2)}
-            order = [(0, s, k) for s in range(PASSES) for k in range(2)] + [(1, s, k) for k in range(2) for s in range(PASSES)]
+        def multiply(e, acc, order):
             for m, s, k in order:
                 nc.tensor.matmul_mx(
                     out=acc[k, m][:],
@@ -112,7 +106,6 @@ def tile_moe_sdn_glu_gelu_kernel(tc, x_words, x_scales, w1_words, w1_scales, w3_
                     start=(s == 0),
                     stop=(s == PASSES - 1),
                 )
-            return acc
 
         def hidden(acc, k, tag):
             act = keep.tile([P, H], F32, name=f"act{k}", tag=f"act{k}", align_bytes=64)
@@ -121,10 +114,27 @@ def tile_moe_sdn_glu_gelu_kernel(tc, x_words, x_scales, w1_words, w1_scales, w3_
             nc.vector.scalar_tensor_tensor(c_slots[:], act[:], gcol[:, k : k + 1], acc[k % 2, 1][:], MULT, MULT)
             return c_slots
 
-        def turn(c_slots, dst):
-            words = c_slots[:].bitcast(F32)
-            for u in range(2):
-                nc.tensor.transpose(dst[:, u, :], words[:, u : H // 2 : 2], ident[:])
+        def hidden_halves(acc, k, order):
+            act = keep.tile([P, H], F32, name=f"act{k}", tag=f"act{k}", align_bytes=64)
+            nc.scalar.activation(act[:], acc[k, 0][:], GELU)
+            pairs = {}
+            for u in order:
+                pairs[u] = keep.tile([P, P, 2], BF16, name=f"pairs{k}{u}", align_bytes=64)
+                nc.vector.scalar_tensor_tensor(pairs[u][:], plane_of(act[:], u), gcol[:, k : k + 1], plane_of(acc[k, 1][:], u), MULT, MULT)
+            return pairs
+
+        def plane_of(ap, u):
+            return ap.rearrange("p (q u d) -> p u q d", u=2, d=2)[:, u]
+
+        def turn_half(pairs, j):
+            dst = bank(j, P)
+            nc.tensor.transpose(dst[:], pairs[:].rearrange("p q d -> p (q d)").bitcast(F32), ident[:])
+            return dst
+
+        def turn(c_slots, u, j):
+            dst = bank(j, P)
+            nc.tensor.transpose(dst[:], c_slots[:].bitcast(F32)[:, u : H // 2 : 2], ident[:])
+            return dst
 
         def scatter(u, lst, src):
             nc.vector.tensor_copy(planes[u][:].indirect(lst), src)
@@ -132,31 +142,56 @@ def tile_moe_sdn_glu_gelu_kernel(tc, x_words, x_scales, w1_words, w1_scales, w3_
         for s in range(PASSES):
             gather_words(0, s)
             gather_scales(0, s, keep.tile([P, C], U8, name=f"gs0{s}", align_bytes=64))
-        for s in range(PASSES):
-            gather_words(1, s)
+        for h in range(2):
+            nc.sync.dma_start(xs[32 * h + 4 : 32 * h + 20, :T].bitcast(I32), x_scales[1:3, 8 * h : 8 * h + 8, :].rearrange("s b t -> b s t").bitcast(I32))
+        load_words(0, 1)
+        load_scales(0, 1, range(3))
+        with nc.allow_non_contiguous_dma(reason="one gate value a partition"):
+            nc.sync.dma_start(gcol[:], gate[0:1, :].rearrange("o (k p) -> p (o k)", p=P))
+        load_scales(0, 1, range(3, 4))
+        load_scales(1, 1, range(1))
+        load_words(1, 1)
+        load_scales(1, 1, range(1, 4))
         for s in range(PASSES - 1):
-            gather_scales(1, s, early.tile([P, C], U8, name=f"gs1{s}", offset=s * C, align_bytes=64))
+            gather_words(1, s)
+        packed = keep.tile([P, C], U8, name="packed", align_bytes=64)
+        gather_scales(1, 0, packed)
+        for q in range(4):
+            row = 32 * (q // 2) + 4 + 8 * (q % 2)
+            nc.sync.dma_start(moved_scales[32 * q : 32 * q + 4].bitcast(I32), packed[row : row + 8].bitcast(I32))
+        for s in (1, 2):
+            gs[1, s] = moved_scales[:, s - 1]
+        gather_words(1, PASSES - 1)
+        w2rows = w2.rearrange("(p j) n -> p j n", j=4)
+        w2raw = [late.tile([P, 4, N // 2], F32, name=f"w2raw{b}", offset=8 * N * (1 - b), align_bytes=64) for b in range(2)]
+        for b in range(2):
+            nc.sync.dma_start(w2raw[b][:], w2rows[:, :, b * N // 2 : (b + 1) * N // 2])
 
-        acc = first_layer(0)
-        rows = [hidden(acc, 0, "c0"), hidden(acc, 1, "c1")]
+        acc = {(k, m): bank(2 * m + k, H) for m in range(2) for k in range(2)}
+        multiply(0, acc, [(0, s, k) for s in range(PASSES) for k in range(2)] + [(1, s, k) for k in range(2) for s in range(PASSES)])
+        rows = [hidden_halves(acc, 0, (1, 0)), hidden_halves(acc, 1, (0, 1))]
         planes = [keep.tile([P, T], F32, name=f"plane{u}") for u in range(2)]
         low = keep.tile([P, C], F32, name="low0")
         high = keep.tile([P, P], F32, name="high0")
-        turned = [psum_tr.tile([P, 2, P], F32, name="tr", tag=f"tr{i}") for i in range(2)]
-        for i in range(2):
-            turn(rows[i], turned[i])
-        gather_scales(1, PASSES - 1, keep.tile([P, C], U8, name="gs12", tag="act0", align_bytes=64))
-        nc.scalar.copy(high[:], turned[0][:, 1, :])
+        nc.scalar.copy(high[:], turn_half(rows[0][1], 6)[:])
         scatter(1, slots(0, 1), high[:])
-        for i in range(2):
-            nc.scalar.copy(low[:, i * P : (i + 1) * P], turned[i][:, 0, :])
+        nc.scalar.copy(low[:, :P], turn_half(rows[0][0], 2)[:])
+        nc.scalar.copy(low[:, P:], turn_half(rows[1][0], 7)[:])
+        kept = turn_half(rows[1][1], 3)
         scatter(0, slots(0, 2), low[:])
 
-        acc = first_layer(1)
-        rows = [hidden(acc, 2, "c2"), hidden(acc, 3, "c3")]
+        acc = {(0, 0): bank(4, H), (1, 0): bank(5, H), (0, 1): bank(0, H)}
+        multiply(1, acc, [(0, 0, 0), (0, 0, 1), (1, 0, 0)] + [(m, s, 0) for m in range(2) for s in (1, 2)] + [(0, s, 1) for s in (1, 2)])
+        rows = [hidden(acc, 2, "c2")]
+        acc[1, 1] = bank(4, H)
+        multiply(1, acc, [(1, s, 1) for s in range(PASSES)])
+        held = words.tile([P, P], F32, name="held", offset=WORDS, align_bytes=64)
+        nc.scalar.copy(held[:], kept[:])
+        scatter(1, slots(1, 2), held[:])
+        rows.append(hidden(acc, 3, "c3"))
 
         def cast_w2(b):
-            w2b = keep.tile([P, N // 2, 4], BF16, name=f"w2b{b}", tag=f"w2b{b}", align_bytes=64)
+            w2b = keep.tile([P, N // 2, 4], BF16, name=f"w2b{b}", tag=("w2b0", "act3")[b], align_bytes=64)
             for c in range(0, N // 2, P):
                 nc.scalar.copy(
                     w2b[:, c : c + P, :].rearrange("p (c i) j -> p c j i", i=4),
@@ -171,29 +206,27 @@ def tile_moe_sdn_glu_gelu_kernel(tc, x_words, x_scales, w1_words, w1_scales, w3_
 
         w2q = []
         w2s = []
-        held = words.tile([P, P], F32, name="held", offset=3 * WORDS, align_bytes=64)
-        nc.scalar.copy(held[:], turned[1][:, 1, :])
-        w2b = [cast_w2(b) for b in range(2)]
-        scatter(1, slots(1, 2), held[:])
-        turned = [psum_tr.tile([P, 2, P], F32, name="tr", tag=f"tr{i}") for i in range(2)]
-        low = late.tile([P, C], F32, name="low1", offset=0, align_bytes=64)
+        w2b = [cast_w2(0)]
+        low = keep.tile([P, C], F32, name="low1", align_bytes=64)
+        turned = []
         for i in range(2):
-            turn(rows[i], turned[i])
-            nc.scalar.copy(low[:, i * P : (i + 1) * P], turned[i][:, 0, :])
+            nc.scalar.copy(low[:, i * P : (i + 1) * P], turn(rows[i], 0, (1, 5)[i])[:])
+            turned.append(turn(rows[i], 1, 6 + i))
+        w2b.append(cast_w2(1))
         scatter(0, slots(2, 3), low[:, :P])
         quantise_w2(0, w2b[0], keep.tile([P, N // 2], U8, name="w2s0", tag="c3", align_bytes=64))
         scatter(0, slots(3, 4), low[:, P:])
         high = keep.tile([P, C], F32, name="high1", tag="w2b0", align_bytes=64)
         for i in range(2):
-            nc.scalar.copy(high[:, i * P : (i + 1) * P], turned[i][:, 1, :])
+            nc.scalar.copy(high[:, i * P : (i + 1) * P], turned[i][:])
 
-        idle = psum_tr.tile([P, H], F32, name="idle", tag="tr1")
+        idle = bank(7, H)
         for r in range(WARM_PASSES):
             nc.tensor.matmul_mx(
                 out=idle[:], lhsT=w2q[0][:, 0:P].bitcast(FP8X4), lhsT_scale=w2s[0][:, 0:P],
-                rhs=ww[0][1][:, 0, :].bitcast(FP4X4), rhs_scale=ws[0][1][:, 0, :], start=True, stop=True,
+                rhs=ww[0][0][:, 0, :].bitcast(FP4X4), rhs_scale=ws[0][0][:, 0, :], start=True, stop=True,
             )
-        cb = [keep.tile([P, HALF, 2], F32, name=f"cb{h}", align_bytes=64) for h in range(2)]
+        cb = [late.tile([P, HALF, 2], F32, name=f"cb{h}", offset=8 * HALF * h, align_bytes=64) for h in range(2)]
         for h in range(2):
             nc.scalar.copy(cb[h][:, :, 0], planes[0][:, h * HALF : (h + 1) * HALF])
         scatter(1, slots(2, 4), high[:])
@@ -212,10 +245,7 @@ def tile_moe_sdn_glu_gelu_kernel(tc, x_words, x_scales, w1_words, w1_scales, w3_
         quantise_c(1, 0, HALF)
         pieces = [(0, 0, P), (1, 0, P), (2, 0, HALF), (3, 0, HALF), (0, P, T), (1, P, T), (2, HALF, T), (3, HALF, T)]
         for j, (a, lo, hi) in enumerate(pieces):
-            if j >= 6:
-                res = psum_tr.tile([P, hi - lo], F32, name="res", tag=f"tr{j - 6}")
-            else:
-                res = psum_acc.tile([P, hi - lo], F32, name="acc")
+            res = bank(j, hi - lo)
             part = slice(a % 2 * P, (a % 2 + 1) * P)
             for h in range(2):
                 first, last = max(lo, h * HALF), min(hi, (h + 1) * HALF)

@@ -22,7 +22,6 @@ PASSES = K // 512
 TILES = E * C // P
 HALF = T // 2
 WORDS = PASSES * 2 * H
-WARM_PASSES = 4
 
 
 def tile_moe_sdn_glu_gelu_kernel(tc, x_words, x_scales, w1_words, w1_scales, w3_words, w3_scales, w2, gate, offs, out):
@@ -220,12 +219,6 @@ def tile_moe_sdn_glu_gelu_kernel(tc, x_words, x_scales, w1_words, w1_scales, w3_
         for i in range(2):
             nc.scalar.copy(high[:, i * P : (i + 1) * P], turned[i][:])
 
-        idle = bank(7, H)
-        for r in range(WARM_PASSES):
-            nc.tensor.matmul_mx(
-                out=idle[:], lhsT=w2q[0][:, 0:P].bitcast(FP8X4), lhsT_scale=w2s[0][:, 0:P],
-                rhs=ww[0][0][:, 0, :].bitcast(FP4X4), rhs_scale=ws[0][0][:, 0, :], start=True, stop=True,
-            )
         cb = [late.tile([P, HALF, 2], F32, name=f"cb{h}", offset=8 * HALF * h, align_bytes=64) for h in range(2)]
         for h in range(2):
             nc.scalar.copy(cb[h][:, :, 0], planes[0][:, h * HALF : (h + 1) * HALF])

from contextlib import ExitStack

import concourse.mybir as mybir
from concourse.masks import make_identity

K, T, E, C, H, N = 1536, 512, 2, 256, 512, 512
FLOPS = 2 * (2 * K * H * E * C + H * N * T)

F32 = mybir.dt.float32
BF16 = mybir.dt.bfloat16
I32 = mybir.dt.int32
U32 = mybir.dt.uint32
U16 = mybir.dt.uint16
U8 = mybir.dt.uint8
FP8X4 = mybir.dt.float8_e4m3fn_x4
FP4X4 = mybir.dt.float4_e2m1fn_x4
GELU = mybir.ActivationFunctionType.Gelu_apprx_tanh
MULT = mybir.AluOpType.mult

P = 128
PASSES = K // 512
TILES = E * C // P
HALF = T // 2
WORDS = PASSES * 2 * H


def tile_moe_sdn_glu_gelu_kernel(tc, x_words, x_scales, w1_words, w1_scales, w3_words, w3_scales, w2, gate, offs, out):
    nc = tc.nc
    with ExitStack() as ctx:
        keep = ctx.enter_context(tc.tile_pool(name="keep", bufs=1))
        early = ctx.enter_context(tc.tile_pool(name="early", bufs=1))
        late = ctx.enter_context(tc.tile_pool(name="late", bufs=1))
        words = ctx.enter_context(tc.tile_pool(name="words", bufs=1))
        psum = ctx.enter_context(tc.psum_pool(name="psum", bufs=1))

        offsets = keep.tile([P, T // 16], U16, name="offsets")
        xw = keep.tile([P, PASSES * T], I32, name="xw", align_bytes=64)
        xs = early.tile([P, PASSES * T], U8, name="xs", offset=0, align_bytes=64)
        ws = [[keep.tile([P, PASSES, H], U8, name=f"ws{m}{e}", align_bytes=64) for e in range(E)] for m in range(2)]
        ww = [[words.tile([P, PASSES, 2 * H], U8, name=f"ww{m}{e}", offset=(m * E + e) * WORDS, align_bytes=64) for e in range(E)] for m in range(2)]
        moved_scales = keep.tile([P, 2, C], U8, name="moved_scales", align_bytes=64)
        gcol = keep.tile([P, TILES], F32, name="gcol")
        ident = keep.tile([P, P], F32, name="ident")

        nc.gpsimd.memset(xs[:].bitcast(I32), 0)
        for e in range(E):
            for m in range(2):
                nc.vector.memset(ws[m][e][:].bitcast(I32), 0)
        nc.vector.memset(moved_scales[:].bitcast(I32), 0)
        make_identity(nc, ident[:])

        def load_tokens(lo, hi):
            nc.sync.dma_start(
                xw[:, lo * T : hi * T].rearrange("p (s t) -> p s t", t=T),
                x_words[lo:hi].rearrange("s p t d -> p s (t d)").bitcast(I32),
            )

        def load_words(m, e):
            nc.sync.dma_start(ww[m][e][:].bitcast(I32), (w1_words, w3_words)[m][e].rearrange("s p b -> p s b").bitcast(I32))

        def load_scales(m, e, rows=range(4)):
            for r in rows:
                nc.sync.dma_start(ws[m][e][r:P:32].bitcast(I32), (w1_scales, w3_scales)[m][e, :, r:16:4, :].rearrange("s q i -> q s i").bitcast(I32))

        load_tokens(0, 1)
        nc.sync.dma_start(offsets[:], offs)
        for r in range(4):
            nc.sync.dma_start(xs[r:P:32].bitcast(I32).rearrange("q (s t) -> q s t", s=PASSES), x_scales[:, r:16:4, :].rearrange("s q t -> q s t").bitcast(I32))
        load_words(0, 0)
        load_scales(0, 0)
        load_tokens(1, 2)
        load_tokens(2, 3)
        load_words(1, 0)
        load_scales(1, 0)

        gw = {}
        gs = {}

        def slots(lo, hi):
            return offsets[:, lo * P // 16 : hi * P // 16]

        def bank(j, width):
            return psum.tile([P, width], F32, name=f"bank{j}", tag=f"bank{j}")

        def gather_words(e, s):
            end = (s + 1) * T if e == 0 else PASSES * T
            if (e, s) == (1, PASSES - 1):
                gw[e, s] = early.tile([P, C], U32, name="gw_last", offset=0, align_bytes=64)
            else:
                gw[e, s] = keep.tile([P, C], U32, name=f"gw{e}{s}", align_bytes=64)
            nc.vector.tensor_copy(gw[e, s][:], xw[:, s * T : end].bitcast(U32).indirect(slots(2 * e, 2 * e + 2)))

        def gather_scales(e, s, dst):
            gs[e, s] = dst
            nc.vector.tensor_copy(dst[:], xs[:, s * T : (s + 1) * T].indirect(slots(2 * e, 2 * e + 2)))

        def multiply(e, acc, order):
            for m, s, k in order:
                nc.tensor.matmul_mx(
                    out=acc[k, m][:],
                    lhsT=gw[e, s][:, k * P : (k + 1) * P].bitcast(FP8X4),
                    lhsT_scale=gs[e, s][:, k * P : (k + 1) * P],
                    rhs=ww[m][e][:, s, :].bitcast(FP4X4),
                    rhs_scale=ws[m][e][:, s, :],
                    start=(s == 0),
                    stop=(s == PASSES - 1),
                )

        def hidden(acc, k, tag):
            act = keep.tile([P, H], F32, name=f"act{k}", tag=f"act{k}", align_bytes=64)
            nc.scalar.activation(act[:], acc[k % 2, 0][:], GELU)
            c_slots = keep.tile([P, H], BF16, name=f"c_slots{k}", tag=tag, align_bytes=64)
            nc.vector.scalar_tensor_tensor(c_slots[:], act[:], gcol[:, k : k + 1], acc[k % 2, 1][:], MULT, MULT)
            return c_slots

        def hidden_halves(acc, k, order):
            act = keep.tile([P, H], F32, name=f"act{k}", tag=f"act{k}", align_bytes=64)
            nc.scalar.activation(act[:], acc[k, 0][:], GELU)
            pairs = {}
            for u in order:
                pairs[u] = keep.tile([P, P, 2], BF16, name=f"pairs{k}{u}", align_bytes=64)
                nc.vector.scalar_tensor_tensor(pairs[u][:], plane_of(act[:], u), gcol[:, k : k + 1], plane_of(acc[k, 1][:], u), MULT, MULT)
            return pairs

        def plane_of(ap, u):
            return ap.rearrange("p (q u d) -> p u q d", u=2, d=2)[:, u]

        def turn_half(pairs, j):
            dst = bank(j, P)
            nc.tensor.transpose(dst[:], pairs[:].rearrange("p q d -> p (q d)").bitcast(F32), ident[:])
            return dst

        def turn(c_slots, u, j):
            dst = bank(j, P)
            nc.tensor.transpose(dst[:], c_slots[:].bitcast(F32)[:, u : H // 2 : 2], ident[:])
            return dst

        def scatter(u, lst, src):
            nc.vector.tensor_copy(planes[u][:].indirect(lst), src)

        for s in range(PASSES):
            gather_words(0, s)
            gather_scales(0, s, keep.tile([P, C], U8, name=f"gs0{s}", align_bytes=64))
        for h in range(2):
            nc.sync.dma_start(xs[32 * h + 4 : 32 * h + 20, :T].bitcast(I32), x_scales[1:3, 8 * h : 8 * h + 8, :].rearrange("s b t -> b s t").bitcast(I32))
        load_words(0, 1)
        load_scales(0, 1, range(3))
        with nc.allow_non_contiguous_dma(reason="one gate value a partition"):
            nc.sync.dma_start(gcol[:], gate[0:1, :].rearrange("o (k p) -> p (o k)", p=P))
        load_scales(0, 1, range(3, 4))
        load_scales(1, 1, range(1))
        load_words(1, 1)
        load_scales(1, 1, range(1, 4))
        for s in range(PASSES - 1):
            gather_words(1, s)
        packed = keep.tile([P, C], U8, name="packed", align_bytes=64)
        gather_scales(1, 0, packed)
        for q in range(4):
            row = 32 * (q // 2) + 4 + 8 * (q % 2)
            nc.sync.dma_start(moved_scales[32 * q : 32 * q + 4].bitcast(I32), packed[row : row + 8].bitcast(I32))
        for s in (1, 2):
            gs[1, s] = moved_scales[:, s - 1]
        gather_words(1, PASSES - 1)
        w2rows = w2.rearrange("(p j) n -> p j n", j=4)
        w2raw = [late.tile([P, 4, N // 2], F32, name=f"w2raw{b}", offset=8 * N * (1 - b), align_bytes=64) for b in range(2)]
        for b in range(2):
            nc.sync.dma_start(w2raw[b][:], w2rows[:, :, b * N // 2 : (b + 1) * N // 2])

        acc = {(k, m): bank(2 * m + k, H) for m in range(2) for k in range(2)}
        multiply(0, acc, [(0, s, k) for s in range(PASSES) for k in range(2)] + [(1, s, k) for k in range(2) for s in range(PASSES)])
        rows = [hidden_halves(acc, 0, (1, 0)), hidden_halves(acc, 1, (0, 1))]
        planes = [keep.tile([P, T], F32, name=f"plane{u}") for u in range(2)]
        low = keep.tile([P, C], F32, name="low0")
        high = keep.tile([P, P], F32, name="high0")
        nc.scalar.copy(high[:], turn_half(rows[0][1], 6)[:])
        scatter(1, slots(0, 1), high[:])
        nc.scalar.copy(low[:, :P], turn_half(rows[0][0], 2)[:])
        nc.scalar.copy(low[:, P:], turn_half(rows[1][0], 7)[:])
        kept = turn_half(rows[1][1], 3)
        scatter(0, slots(0, 2), low[:])

        acc = {(0, 0): bank(4, H), (1, 0): bank(5, H), (0, 1): bank(0, H)}
        multiply(1, acc, [(0, 0, 0), (0, 0, 1), (1, 0, 0)] + [(m, s, 0) for m in range(2) for s in (1, 2)] + [(0, s, 1) for s in (1, 2)])
        rows = [hidden(acc, 2, "c2")]
        acc[1, 1] = bank(4, H)
        multiply(1, acc, [(1, s, 1) for s in range(PASSES)])
        held = words.tile([P, P], F32, name="held", offset=WORDS, align_bytes=64)
        nc.scalar.copy(held[:], kept[:])
        scatter(1, slots(1, 2), held[:])
        rows.append(hidden(acc, 3, "c3"))

        def cast_w2(b):
            w2b = keep.tile([P, N // 2, 4], BF16, name=f"w2b{b}", tag=("w2b0", "act3")[b], align_bytes=64)
            for c in range(0, N // 2, P):
                nc.scalar.copy(
                    w2b[:, c : c + P, :].rearrange("p (c i) j -> p c j i", i=4),
                    w2raw[b][:, :, c : c + P].rearrange("p j (c i) -> p c j i", i=4),
                )
            return w2b

        def quantise_w2(b, w2b, scales):
            w2q.append(keep.tile([P, N // 2], U32, name=f"w2q{b}", align_bytes=64))
            w2s.append(scales)
            nc.vector.quantize_mx(out=w2q[b][:].bitcast(FP8X4), scales=w2s[b][:], in_=w2b[:].rearrange("p n j -> p (n j)"))

        w2q = []
        w2s = []
        w2b = [cast_w2(0)]
        low = keep.tile([P, C], F32, name="low1", align_bytes=64)
        turned = []
        for i in range(2):
            nc.scalar.copy(low[:, i * P : (i + 1) * P], turn(rows[i], 0, (1, 5)[i])[:])
            turned.append(turn(rows[i], 1, 6 + i))
        w2b.append(cast_w2(1))
        scatter(0, slots(2, 3), low[:, :P])
        quantise_w2(0, w2b[0], keep.tile([P, N // 2], U8, name="w2s0", tag="c3", align_bytes=64))
        scatter(0, slots(3, 4), low[:, P:])
        high = keep.tile([P, C], F32, name="high1", tag="w2b0", align_bytes=64)
        for i in range(2):
            nc.scalar.copy(high[:, i * P : (i + 1) * P], turned[i][:])

        cb = [late.tile([P, HALF, 2], F32, name=f"cb{h}", offset=8 * HALF * h, align_bytes=64) for h in range(2)]
        for h in range(2):
            nc.scalar.copy(cb[h][:, :, 0], planes[0][:, h * HALF : (h + 1) * HALF])
        scatter(1, slots(2, 4), high[:])
        for lo in (0, P):
            nc.vector.tensor_copy(cb[0][:, lo : lo + P, 1], planes[1][:, lo : lo + P])
        nc.scalar.copy(cb[1][:, :, 1], planes[1][:, HALF:])
        cq = [keep.tile([P, HALF], U32, name=f"cq{h}", align_bytes=64) for h in range(2)]
        cs = [keep.tile([P, HALF], U8, name=f"cs{h}", align_bytes=64) for h in range(2)]

        def quantise_c(h, lo, hi):
            nc.vector.quantize_mx(out=cq[h][:, lo:hi].bitcast(FP8X4), scales=cs[h][:, lo:hi], in_=cb[h][:, lo:hi, :].rearrange("p t u -> p (t u)").bitcast(BF16))

        quantise_c(0, 0, P)
        quantise_c(0, P, HALF)
        quantise_w2(1, w2b[1], keep.tile([P, N // 2], U8, name="w2s1", tag="w2b0", align_bytes=64))
        quantise_c(1, 0, HALF)
        pieces = [(0, 0, P), (1, 0, P), (2, 0, HALF), (3, 0, HALF), (0, P, T), (1, P, T), (2, HALF, T), (3, HALF, T)]
        for j, (a, lo, hi) in enumerate(pieces):
            res = bank(j, hi - lo)
            part = slice(a % 2 * P, (a % 2 + 1) * P)
            for h in range(2):
                first, last = max(lo, h * HALF), min(hi, (h + 1) * HALF)
                if first < last:
                    nc.tensor.matmul_mx(
                        out=res[:, first - lo : last - lo],
                        lhsT=w2q[a // 2][:, part].bitcast(FP8X4),
                        lhsT_scale=w2s[a // 2][:, part],
                        rhs=cq[h][:, first - h * HALF : last - h * HALF].bitcast(FP8X4),
                        rhs_scale=cs[h][:, first - h * HALF : last - h * HALF],
                        start=True,
                        stop=True,
                    )
            staged = keep.tile([P, hi - lo], F32, name=f"staged{j}")
            if j % 2 == 0:
                nc.scalar.copy(staged[:], res[:])
            else:
                nc.vector.tensor_copy(staged[:], res[:])
            nc.sync.dma_start(out[a * P : (a + 1) * P, lo:hi], staged[:])
